import numpy as np
import ml_dtypes


def mxq(x, axis, fmt="e4m3"):
    dtype, down = {"e4m3": (ml_dtypes.float8_e4m3fn, 7), "e5m2": (ml_dtypes.float8_e5m2, 14)}[fmt]
    v = np.moveaxis(np.asarray(x, np.float32).astype(ml_dtypes.bfloat16).astype(np.float64), axis, -1)
    blocks = v.reshape(v.shape[:-1] + (-1, 32))
    amax = np.abs(blocks).max(-1, keepdims=True)
    byte = np.maximum(np.where(amax > 0, np.frexp(amax)[1] - 1 + 127, 0) - down, 1)
    scale = np.exp2(byte - 127.0)
    codes = (blocks / scale).astype(np.float32).astype(dtype).astype(np.float64)
    return np.moveaxis((codes * scale).reshape(v.shape), -1, axis)


WIDE = False


def mx_kscale(k):
    if not WIDE:
        return np.ones(k)
    levels = np.array([24, -24, 12, -12, 0])
    if k % 512:
        return np.exp2(np.random.permutation(np.resize(levels, k // 32))).repeat(32)
    a = np.empty((k // 512, 16))
    for p in range(k // 512):
        a[p, :8] = np.random.permutation(np.resize(levels, 8))
        for g in range(8):
            far = levels[np.abs(levels - a[p, g]) >= 10]
            a[p, g + 8] = far[np.random.randint(len(far))]
    return np.exp2(a.ravel()).repeat(32)


def f64(x):
    return np.asarray(x).astype(np.float64)


def striped(idx):
    return np.tile(idx.reshape(-1, 16).T, (8, 1)).astype(np.uint16)


def unstriped(offs):
    return offs[:16].T.reshape(-1).astype(np.int64)


def striped8(idx):
    return np.concatenate([v.reshape(-1, 16).T for v in idx]).astype(np.uint16)


def unstriped8(offs):
    return np.stack([offs[16 * g:16 * g + 16].T.reshape(-1) for g in range(8)]).astype(np.int64)


E2M1 = np.array([0.0, 0.5, 1.0, 1.5, 2.0, 3.0, 4.0, 6.0, -0.0, -0.5, -1.0, -1.5, -2.0, -3.0, -4.0, -6.0])


def pack_weight(w, fmt):
    k, n = w.shape
    w = f64(np.asarray(w, np.float32).astype(ml_dtypes.bfloat16)).reshape(k // 32, 32, n)
    amax = np.abs(w).max(1)
    if fmt == "e4m3":
        byte = np.frexp(amax)[1] - 1 + 127 - 7
    else:
        mant, ex = np.frexp(amax / 6.0)
        byte = np.where(mant > 0.5, ex, ex - 1) + 127
    byte = np.clip(np.where(amax > 0, byte, 1), 1, 254)
    scaled = (w * np.exp2(127.0 - byte)[:, None, :]).reshape(k, n).astype(np.float32)
    by_word = np.ascontiguousarray(scaled.reshape(k // 512, 128, 4, n).transpose(0, 1, 3, 2))
    if fmt == "e4m3":
        words = by_word.astype(ml_dtypes.float8_e4m3fn).view(np.uint8)
    else:
        c = by_word.astype(ml_dtypes.float4_e2m1fn).view(np.uint8) & 0xF
        words = (c[..., 0::2] | (c[..., 1::2] << 4)).reshape(k // 512, 128, 2 * n)
    return np.ascontiguousarray(words), np.ascontiguousarray(byte.astype(np.uint8).reshape(k // 512, 16, n))


def unpack_weight(words, scales, fmt):
    g, _, n = scales.shape
    words = np.ascontiguousarray(words).reshape(g, 128, n, -1)
    if fmt == "e4m3":
        vals = words.view(ml_dtypes.float8_e4m3fn).astype(np.float64)
    else:
        nib = np.empty((g, 128, n, 4), np.uint8)
        nib[..., 0::2] = words & 0xF
        nib[..., 1::2] = words >> 4
        vals = E2M1[nib]
    vals = vals * np.repeat(np.exp2(scales.astype(np.float64) - 127.0), 8, axis=1)[..., None]
    return vals.transpose(0, 1, 3, 2).reshape(g * 512, n)


K, L, R, N, T, J = 512, 512, 512, 512, 2048, 1024


def setup_inputs():
    n = np.random.standard_normal
    s = mx_kscale(K)[:, None]
    s2 = mx_kscale(L)[:, None]
    u = mx_kscale(R)[:, None]
    p_tab = pack_weight(n((L, T)) * s2, "e4m3")
    p_wa = pack_weight(n((K, R)) / np.sqrt(K) / s * u.T, "e4m3")
    p_wd = pack_weight(n((R, N)) / np.sqrt(R) / u, "e2m1")
    return {
        "tab_words": p_tab[0],
        "tab_scales": p_tab[1],
        "xT": (n((K, T)) * s).astype(np.float32),
        "wgt2": np.repeat(np.random.uniform(0.5, 2.0, (8, J)), 16, axis=0).astype(np.float32),
        "wa_words": p_wa[0],
        "wa_scales": p_wa[1],
        "wb": (n((L, R)) / np.sqrt(L) / s2 * u.T).astype(np.float32),
        "wd_words": p_wd[0],
        "wd_scales": p_wd[1],
        "gT": (n((N, T))).astype(np.float32),
        "offs": striped(np.random.permutation(T)[:J]),
        "offs2": striped8(np.stack([np.random.permutation(T)[:J] for _ in range(8)])),
    }


def reference(tab_words, tab_scales, xT, wgt2, wa_words, wa_scales, wb, wd_words, wd_scales, gT, offs, offs2):
    idx = unstriped(offs)
    idx2 = unstriped8(offs2)
    tab_ = unpack_weight(tab_words, tab_scales, "e4m3")[:, idx]
    rows = np.arange(K)
    xg = f64(wgt2)[rows // 4 % 128] * f64(xT)[rows[:, None], idx2[rows % 512 // 64]]
    xT_ = mxq(xg, 0, "e4m3")
    wa_ = unpack_weight(wa_words, wa_scales, "e4m3")
    wb_ = mxq(f64(wb), 0, "e4m3")
    ya = wa_.T @ xT_
    yb = wb_.T @ tab_
    h = np.maximum(ya, yb)
    h_ = mxq(h, 0, "e4m3")
    wd_ = unpack_weight(wd_words, wd_scales, "e2m1")
    y = wd_.T @ h_
    return y * f64(gT)[:, idx]

@@ -1,0 +1,203 @@
+from contextlib import ExitStack
+
+import concourse.mybir as mybir
+
+K, L, R, N, T, J = 512, 512, 512, 512, 2048, 1024
+FLOPS = 2 * J * (K * R + L * R + R * N)
+
+F32 = mybir.dt.float32
+BF16 = mybir.dt.bfloat16
+I32 = mybir.dt.int32
+U32 = mybir.dt.uint32
+U16 = mybir.dt.uint16
+U8 = mybir.dt.uint8
+FP8X4 = mybir.dt.float8_e4m3fn_x4
+FP4X4 = mybir.dt.float4_e2m1fn_x4
+MULT = mybir.AluOpType.mult
+MAX = mybir.AluOpType.max
+
+P = 128
+PACK = 4
+STRIPE = 16
+PART = 256
+PARTS = J // PART
+BANK_J = 128
+
+
+def load_scale_rows(queue, plane, rows):
+    for q in range(4):
+        queue.dma_start(out=plane[32 * q : 32 * q + 4, :].bitcast(I32), in_=rows[0, 4 * q : 4 * q + 4, :].bitcast(I32))
+
+
+def tile_list_htabg_max_gateL_kernel(
+    tc, tab_words, tab_scales, xT, wgt2, wa_words, wa_scales, wb, wd_words, wd_scales, gT, offs, offs2, out
+):
+    nc = tc.nc
+    with ExitStack() as ctx:
+        lists = ctx.enter_context(tc.tile_pool(name="lists", bufs=1))
+        keep = ctx.enter_context(tc.tile_pool(name="keep", bufs=1))
+        psum = ctx.enter_context(tc.psum_pool(name="psum", bufs=4))
+
+        def tile(name, shape, dtype):
+            return keep.tile(shape, dtype, name=name, align_bytes=64)
+
+        idx = lists.tile([P, J // STRIPE], U16, name="idx")
+        idx2 = lists.tile([P, J // STRIPE], U16, name="idx2")
+
+        tab_s = tile("tab_s", [P, T], U8)
+        wa_s_raw = tile("wa_s_raw", [P, R], U8)
+        wd_s = tile("wd_s", [P, N], U8)
+        for plane in (tab_s, wa_s_raw, wd_s):
+            nc.vector.memset(plane[:].bitcast(I32), 0)
+
+        nc.sync.dma_start(idx[:], offs)
+        wa_w_raw = tile("wa_w_raw", [P, R], I32)
+        nc.sync.dma_start(out=wa_w_raw[:], in_=wa_words[0].rearrange("p r i -> p (r i)").bitcast(I32))
+        wb_raw = tile("wb_raw", [P, PACK, R], F32)
+        nc.sync.dma_start(out=wb_raw[:], in_=wb.rearrange("(p i) r -> p i r", i=PACK))
+        load_scale_rows(nc.sync, tab_s, tab_scales)
+        tab_w = tile("tab_w", [P, T], I32)
+        nc.sync.dma_start(out=tab_w[:], in_=tab_words[0].rearrange("p t i -> p (t i)").bitcast(I32))
+        load_scale_rows(nc.sync, wa_s_raw, wa_scales)
+        nc.sync.dma_start(idx2[:], offs2)
+        wgt = tile("wgt", [P, J], F32)
+        nc.sync.dma_start(out=wgt[:], in_=wgt2)
+        x_rows = xT.rearrange("(p i) t -> p i t", i=PACK)
+        x_planes = []
+        for i in range(PACK):
+            plane = tile(f"x{i}", [P, T], F32)
+            nc.sync.dma_start(out=plane[:], in_=x_rows[:, i, :])
+            x_planes.append(plane)
+        wd_w = tile("wd_w", [P, 2 * N], U8)
+        nc.sync.dma_start(out=wd_w[:].bitcast(I32), in_=wd_words[0].bitcast(I32))
+        load_scale_rows(nc.sync, wd_s, wd_scales)
+        gates = []
+        for b in range(N // P):
+            gate = tile(f"g{b}", [P, T], F32)
+            nc.sync.dma_start(out=gate[:], in_=gT[b * P : (b + 1) * P, :])
+            gates.append(gate)
+
+        v_s = tile("v_s", [P, J], U8)
+        nc.vector.tensor_copy(v_s[:], tab_s[:].indirect(idx[:]))
+
+        wa_w = tile("wa_w", [P, R], I32)
+        nc.vector.tensor_copy(
+            out=wa_w[:].rearrange("p (t m) -> p m t", t=PACK), in_=wa_w_raw[:].rearrange("p (m t) -> p m t", t=PACK)
+        )
+        wa_s = tile("wa_s", [P, R], U8)
+        nc.vector.tensor_copy(
+            out=wa_s[:].rearrange("p (t m) -> p m t", t=PACK), in_=wa_s_raw[:].rearrange("p (m t) -> p m t", t=PACK)
+        )
+
+        wb_bf = tile("wb_bf", [P, PACK * R], BF16)
+        nc.scalar.copy(
+            out=wb_bf[:].rearrange("p (t m i) -> p m i t", t=PACK, i=PACK),
+            in_=wb_raw[:].rearrange("p i (m t) -> p m i t", t=PACK),
+        )
+        v_w = tile("v_w", [P, J], U32)
+        nc.vector.tensor_copy(v_w[:], tab_w[:].bitcast(U32).indirect(idx[:]))
+        wb_w = tile("wb_w", [P, R], U32)
+        wb_s = tile("wb_s", [P, R], U8)
+        nc.vector.quantize_mx(out=wb_w[:].bitcast(FP8X4), scales=wb_s[:], in_=wb_bf[:])
+
+        def project(name, w_words, w_scales, words, scales):
+            rounded = tile(name, [P, PART, PACK], BF16)
+            for j0 in range(0, PART, BANK_J):
+                cols = slice(j0, j0 + BANK_J)
+                bank = psum.tile([P, PACK, BANK_J], F32, name="first")
+                for t in range(PACK):
+                    rows = slice(t * P, (t + 1) * P)
+                    nc.tensor.matmul_mx(
+                        out=bank[:, t, :],
+                        lhsT=w_words[:, rows].bitcast(FP8X4),
+                        lhsT_scale=w_scales[:, rows],
+                        rhs=words[:, cols].bitcast(FP8X4),
+                        rhs_scale=scales[:, cols],
+                        start=True,
+                        stop=True,
+                    )
+                nc.scalar.copy(out=rounded[:, cols, :], in_=bank[:].rearrange("p t j -> p j t"))
+            return rounded
+
+        yb = []
+        for c in range(PARTS):
+            cols = slice(c * PART, (c + 1) * PART)
+            yb.append(project(f"yb{c}", wb_w, wb_s, v_w[:, cols], v_s[:, cols]))
+
+        def part_list(offsets, c):
+            return offsets[:, c * PART // STRIPE : (c + 1) * PART // STRIPE]
+
+        picked = [tile(f"xg{c}", [P, PACK, PART], F32) for c in range(PARTS)]
+
+        def pick(i, c):
+            nc.vector.tensor_tensor(
+                picked[c][:, i, :], x_planes[i][:].indirect(part_list(idx2, c)), wgt[:, c * PART : (c + 1) * PART], MULT
+            )
+
+        def quantise(name, values):
+            words = tile(name + "_w", [P, PART], U32)
+            scales = tile(name + "_s", [P, PART], U8)
+            nc.vector.quantize_mx(
+                out=words[:].bitcast(FP8X4), scales=scales[:], in_=values[:].rearrange("p j t -> p (j t)")
+            )
+            return words, scales
+
+        def weave(c):
+            woven = tile(f"xb{c}", [P, PART, PACK], BF16)
+            nc.scalar.copy(
+                out=woven[:].rearrange("p (u v) i -> p u i v", v=4),
+                in_=picked[c][:].rearrange("p i (u v) -> p u i v", v=4),
+            )
+            return woven
+
+        def first_stage(c, woven):
+            words, scales = quantise(f"xq{c}", woven)
+            return project(f"ya{c}", wa_w, wa_s, words[:], scales[:])
+
+        def join(c, ya):
+            h = tile(f"h{c}", [P, PART, PACK], BF16)
+            nc.vector.tensor_tensor(h[:], ya[:], yb[c][:], MAX)
+            return h
+
+        def second_stage(c, h):
+            words, scales = quantise(f"hq{c}", h)
+            y = tile(f"y{c}", [P, N // P, PART], F32)
+            for b0 in range(0, N // P, 2):
+                bank = psum.tile([P, 2, PART], F32, name="second")
+                for e in range(2):
+                    b = b0 + e
+                    nc.tensor.matmul_mx(
+                        out=bank[:, e, :],
+                        lhsT=wd_w[:, 2 * b * P : 2 * (b + 1) * P].bitcast(FP4X4),
+                        lhsT_scale=wd_s[:, b * P : (b + 1) * P],
+                        rhs=words[:].bitcast(FP8X4),
+                        rhs_scale=scales[:],
+                        start=True,
+                        stop=True,
+                    )
+                nc.scalar.copy(out=y[:, b0 : b0 + 2, :], in_=bank[:])
+            return y
+
+        def gate_and_store(c, y):
+            for b in range(N // P):
+                gated = tile(f"o{c}_{b}", [P, PART], F32)
+                nc.vector.tensor_tensor(gated[:], gates[b][:].indirect(part_list(idx, c)), y[:, b, :], MULT)
+                nc.sync.dma_start(out=out[b * P : (b + 1) * P, c * PART : (c + 1) * PART], in_=gated[:])
+
+        for i in range(2):
+            for c in range(PARTS):
+                pick(i, c)
+        woven, ya, h, y = {}, {}, {}, {}
+        for step in range(PARTS + 4):
+            if step < PARTS:
+                pick(2, step)
+                pick(3, step)
+                woven[step] = weave(step)
+            if 0 <= step - 1 < PARTS:
+                ya[step - 1] = first_stage(step - 1, woven[step - 1])
+            if 0 <= step - 2 < PARTS:
+                h[step - 2] = join(step - 2, ya[step - 2])
+            if 0 <= step - 3 < PARTS:
+                y[step - 3] = second_stage(step - 3, h[step - 3])
+            if 0 <= step - 4 < PARTS:
+                gate_and_store(step - 4, y[step - 4])

@@ -19,14 +19,22 @@ MAX = mybir.AluOpType.max
 P = 128
 PACK = 4
 STRIPE = 16
-PART = 256
+PART = 128
 PARTS = J // PART
-BANK_J = 128
+LOOKUP = 1024
+GATE = (256, 256, 256, 256)
+STEPS = (128, 128, 128, 128, 256, 256)
+LAST_PICKS = (512, 512)
+DIRECT = 4
 
 
 def load_scale_rows(queue, plane, rows):
     for q in range(4):
         queue.dma_start(out=plane[32 * q : 32 * q + 4, :].bitcast(I32), in_=rows[0, 4 * q : 4 * q + 4, :].bitcast(I32))
+
+
+def entries(offsets, j0, width):
+    return offsets[:, j0 // STRIPE : (j0 + width) // STRIPE]
 
 
 def tile_list_htabg_max_gateL_kernel(
@@ -36,7 +44,8 @@ def tile_list_htabg_max_gateL_kernel(
     with ExitStack() as ctx:
         lists = ctx.enter_context(tc.tile_pool(name="lists", bufs=1))
         keep = ctx.enter_context(tc.tile_pool(name="keep", bufs=1))
-        psum = ctx.enter_context(tc.psum_pool(name="psum", bufs=4))
+        psum1 = ctx.enter_context(tc.psum_pool(name="psum1", bufs=5))
+        psum2 = ctx.enter_context(tc.psum_pool(name="psum2", bufs=3))
 
         def tile(name, shape, dtype):
             return keep.tile(shape, dtype, name=name, align_bytes=64)
@@ -50,43 +59,44 @@ def tile_list_htabg_max_gateL_kernel(
         for plane in (tab_s, wa_s_raw, wd_s):
             nc.vector.memset(plane[:].bitcast(I32), 0)
 
-        nc.sync.dma_start(idx[:], offs)
         wa_w_raw = tile("wa_w_raw", [P, R], I32)
-        nc.sync.dma_start(out=wa_w_raw[:], in_=wa_words[0].rearrange("p r i -> p (r i)").bitcast(I32))
         wb_raw = tile("wb_raw", [P, PACK, R], F32)
-        nc.sync.dma_start(out=wb_raw[:], in_=wb.rearrange("(p i) r -> p i r", i=PACK))
-        load_scale_rows(nc.sync, tab_s, tab_scales)
         tab_w = tile("tab_w", [P, T], I32)
-        nc.sync.dma_start(out=tab_w[:], in_=tab_words[0].rearrange("p t i -> p (t i)").bitcast(I32))
-        load_scale_rows(nc.sync, wa_s_raw, wa_scales)
-        nc.sync.dma_start(idx2[:], offs2)
         wgt = tile("wgt", [P, J], F32)
-        nc.sync.dma_start(out=wgt[:], in_=wgt2)
-        x_rows = xT.rearrange("(p i) t -> p i t", i=PACK)
-        x_planes = []
-        for i in range(PACK):
-            plane = tile(f"x{i}", [P, T], F32)
-            nc.sync.dma_start(out=plane[:], in_=x_rows[:, i, :])
-            x_planes.append(plane)
         wd_w = tile("wd_w", [P, 2 * N], U8)
-        nc.sync.dma_start(out=wd_w[:].bitcast(I32), in_=wd_words[0].bitcast(I32))
+        x_rows = xT.rearrange("(p i) t -> p i t", i=PACK)
+        x_planes = [tile(f"x{i}", [P, T], F32) for i in range(PACK)]
+        gates = [tile(f"g{b}", [P, T], F32) for b in range(N // P)]
+
+        nc.sync.dma_start(idx[:], offs)
+        nc.sync.dma_start(out=tab_w[:], in_=tab_words[0].rearrange("p t i -> p (t i)").bitcast(I32))
+        load_scale_rows(nc.sync, tab_s, tab_scales)
+        nc.sync.dma_start(idx2[:], offs2)
+        nc.sync.dma_start(out=wb_raw[:], in_=wb.rearrange("(p i) r -> p i r", i=PACK))
+        nc.sync.dma_start(out=wa_w_raw[:], in_=wa_words[0].rearrange("p r i -> p (r i)").bitcast(I32))
+        load_scale_rows(nc.sync, wa_s_raw, wa_scales)
+        nc.sync.dma_start(out=wgt[:], in_=wgt2)
+        nc.sync.dma_start(out=x_planes[0][:], in_=x_rows[:, 0, :])
+        nc.sync.dma_start(out=x_planes[1][:], in_=x_rows[:, 1, :])
         load_scale_rows(nc.sync, wd_s, wd_scales)
-        gates = []
-        for b in range(N // P):
-            gate = tile(f"g{b}", [P, T], F32)
-            nc.sync.dma_start(out=gate[:], in_=gT[b * P : (b + 1) * P, :])
-            gates.append(gate)
+        nc.sync.dma_start(out=x_planes[2][:], in_=x_rows[:, 2, :])
+        nc.sync.dma_start(out=x_planes[3][:], in_=x_rows[:, 3, :])
+        nc.sync.dma_start(out=wd_w[:].bitcast(I32), in_=wd_words[0].bitcast(I32))
+        nc.sync.dma_start(out=gates[0][:], in_=gT[0 * P : 1 * P, :])
+        nc.sync.dma_start(out=gates[1][:], in_=gT[1 * P : 2 * P, :])
+        nc.sync.dma_start(out=gates[2][:], in_=gT[2 * P : 3 * P, :])
+        nc.sync.dma_start(out=gates[3][:], in_=gT[3 * P : 4 * P, :])
 
         v_s = tile("v_s", [P, J], U8)
         nc.vector.tensor_copy(v_s[:], tab_s[:].indirect(idx[:]))
 
         wa_w = tile("wa_w", [P, R], I32)
         nc.vector.tensor_copy(
-            out=wa_w[:].rearrange("p (t m) -> p m t", t=PACK), in_=wa_w_raw[:].rearrange("p (m t) -> p m t", t=PACK)
+            out=wa_w[:].rearrange("p (t m) -> p t m", t=PACK), in_=wa_w_raw[:].rearrange("p (m t) -> p t m", t=PACK)
         )
         wa_s = tile("wa_s", [P, R], U8)
         nc.vector.tensor_copy(
-            out=wa_s[:].rearrange("p (t m) -> p m t", t=PACK), in_=wa_s_raw[:].rearrange("p (m t) -> p m t", t=PACK)
+            out=wa_s[:].rearrange("p (t m) -> p t m", t=PACK), in_=wa_s_raw[:].rearrange("p (m t) -> p t m", t=PACK)
         )
 
         wb_bf = tile("wb_bf", [P, PACK * R], BF16)
@@ -94,110 +104,101 @@ def tile_list_htabg_max_gateL_kernel(
             out=wb_bf[:].rearrange("p (t m i) -> p m i t", t=PACK, i=PACK),
             in_=wb_raw[:].rearrange("p i (m t) -> p m i t", t=PACK),
         )
-        v_w = tile("v_w", [P, J], U32)
-        nc.vector.tensor_copy(v_w[:], tab_w[:].bitcast(U32).indirect(idx[:]))
         wb_w = tile("wb_w", [P, R], U32)
         wb_s = tile("wb_s", [P, R], U8)
         nc.vector.quantize_mx(out=wb_w[:].bitcast(FP8X4), scales=wb_s[:], in_=wb_bf[:])
 
-        def project(name, w_words, w_scales, words, scales):
-            rounded = tile(name, [P, PART, PACK], BF16)
-            for j0 in range(0, PART, BANK_J):
-                cols = slice(j0, j0 + BANK_J)
-                bank = psum.tile([P, PACK, BANK_J], F32, name="first")
-                for t in range(PACK):
-                    rows = slice(t * P, (t + 1) * P)
-                    nc.tensor.matmul_mx(
-                        out=bank[:, t, :],
-                        lhsT=w_words[:, rows].bitcast(FP8X4),
-                        lhsT_scale=w_scales[:, rows],
-                        rhs=words[:, cols].bitcast(FP8X4),
-                        rhs_scale=scales[:, cols],
-                        start=True,
-                        stop=True,
-                    )
-                nc.scalar.copy(out=rounded[:, cols, :], in_=bank[:].rearrange("p t j -> p j t"))
-            return rounded
+        picked = tile("picked", [P, PACK, J], F32)
+        for i in range(PACK - 1):
+            nc.vector.tensor_tensor(picked[:, i, :], x_planes[i][:].indirect(idx2[:]), wgt[:], MULT)
 
-        yb = []
-        for c in range(PARTS):
-            cols = slice(c * PART, (c + 1) * PART)
-            yb.append(project(f"yb{c}", wb_w, wb_s, v_w[:, cols], v_s[:, cols]))
+        def project(w_words, w_scales, words, scales):
+            bank = psum1.tile([P, PACK, PART], F32, name="first")
+            for t in range(PACK):
+                rows = slice(t * P, (t + 1) * P)
+                nc.tensor.matmul_mx(
+                    out=bank[:, t, :],
+                    lhsT=w_words[:, rows].bitcast(FP8X4),
+                    lhsT_scale=w_scales[:, rows],
+                    rhs=words.bitcast(FP8X4),
+                    rhs_scale=scales,
+                    start=True,
+                    stop=True,
+                )
+            return bank[:].rearrange("p t j -> p j t")
 
-        def part_list(offsets, c):
-            return offsets[:, c * PART // STRIPE : (c + 1) * PART // STRIPE]
-
-        picked = [tile(f"xg{c}", [P, PACK, PART], F32) for c in range(PARTS)]
-
-        def pick(i, c):
-            nc.vector.tensor_tensor(
-                picked[c][:, i, :], x_planes[i][:].indirect(part_list(idx2, c)), wgt[:, c * PART : (c + 1) * PART], MULT
-            )
 
         def quantise(name, values):
-            words = tile(name + "_w", [P, PART], U32)
-            scales = tile(name + "_s", [P, PART], U8)
+            width = values.shape[1]
+            words = tile(name + "_w", [P, width], U32)
+            scales = tile(name + "_s", [P, width], U8)
             nc.vector.quantize_mx(
                 out=words[:].bitcast(FP8X4), scales=scales[:], in_=values[:].rearrange("p j t -> p (j t)")
             )
             return words, scales
 
-        def weave(c):
-            woven = tile(f"xb{c}", [P, PART, PACK], BF16)
+        v_w = tile("v_w", [P, J], U32)
+        y = tile("y", [P, N // P, J], F32)
+        yb = tile("yb", [P, J, PACK], BF16)
+
+        def look_up(c):
+            cols = slice(c * PART, (c + 1) * PART)
+            if c * PART % LOOKUP == 0:
+                nc.vector.tensor_copy(
+                    v_w[:, c * PART : c * PART + LOOKUP], tab_w[:].bitcast(U32).indirect(entries(idx, c * PART, LOOKUP))
+                )
+            nc.scalar.copy(out=yb[:, cols, :], in_=project(wb_w, wb_s, v_w[:, cols], v_s[:, cols]))
+
+        for c in range(PARTS):
+            look_up(c)
+
+        pick_starts = [sum(LAST_PICKS[:n]) for n in range(len(LAST_PICKS))]
+        j0 = 0
+        for c, width in enumerate(STEPS):
+            for start, count in zip(pick_starts, LAST_PICKS):
+                if j0 <= start < j0 + width:
+                    wide = slice(start, start + count)
+                    nc.vector.tensor_tensor(
+                        picked[:, PACK - 1, wide], x_planes[PACK - 1][:].indirect(entries(idx2, start, count)), wgt[:, wide], MULT
+                    )
+            woven = tile(f"xb{c}", [P, width, PACK], BF16)
             nc.scalar.copy(
                 out=woven[:].rearrange("p (u v) i -> p u i v", v=4),
-                in_=picked[c][:].rearrange("p i (u v) -> p u i v", v=4),
+                in_=picked[:, :, j0 : j0 + width].rearrange("p i (u v) -> p u i v", v=4),
             )
-            return woven
-
-        def first_stage(c, woven):
-            words, scales = quantise(f"xq{c}", woven)
-            return project(f"ya{c}", wa_w, wa_s, words[:], scales[:])
-
-        def join(c, ya):
-            h = tile(f"h{c}", [P, PART, PACK], BF16)
-            nc.vector.tensor_tensor(h[:], ya[:], yb[c][:], MAX)
-            return h
-
-        def second_stage(c, h):
-            words, scales = quantise(f"hq{c}", h)
-            y = tile(f"y{c}", [P, N // P, PART], F32)
-            for b0 in range(0, N // P, 2):
-                bank = psum.tile([P, 2, PART], F32, name="second")
-                for e in range(2):
-                    b = b0 + e
+            x_w, x_s = quantise(f"xq{c}", woven)
+            h = tile(f"h{c}", [P, width, PACK], BF16)
+            if c < DIRECT:
+                for u in range(0, width, PART):
+                    ya = project(wa_w, wa_s, x_w[:, u : u + PART], x_s[:, u : u + PART])
+                    nc.vector.tensor_tensor(h[:, u : u + PART, :], ya, yb[:, j0 + u : j0 + u + PART, :], MAX)
+            else:
+                ya = tile(f"ya{c}", [P, width, PACK], BF16)
+                for u in range(0, width, PART):
+                    nc.scalar.copy(
+                        out=ya[:, u : u + PART, :], in_=project(wa_w, wa_s, x_w[:, u : u + PART], x_s[:, u : u + PART])
+                    )
+                nc.vector.tensor_tensor(h[:], ya[:], yb[:, j0 : j0 + width, :], MAX)
+            h_w, h_s = quantise(f"hq{c}", h)
+            for u in range(0, width, PART):
+                bank = psum2.tile([P, N // P, PART], F32, name="second")
+                for b in range(N // P):
                     nc.tensor.matmul_mx(
-                        out=bank[:, e, :],
+                        out=bank[:, b, :],
                         lhsT=wd_w[:, 2 * b * P : 2 * (b + 1) * P].bitcast(FP4X4),
                         lhsT_scale=wd_s[:, b * P : (b + 1) * P],
-                        rhs=words[:].bitcast(FP8X4),
-                        rhs_scale=scales[:],
+                        rhs=h_w[:, u : u + PART].bitcast(FP8X4),
+                        rhs_scale=h_s[:, u : u + PART],
                         start=True,
                         stop=True,
                     )
-                nc.scalar.copy(out=y[:, b0 : b0 + 2, :], in_=bank[:])
-            return y
+                nc.scalar.copy(out=y[:, :, j0 + u : j0 + u + PART], in_=bank[:])
+            j0 = j0 + width
 
-        def gate_and_store(c, y):
+        j0 = 0
+        for width in GATE:
             for b in range(N // P):
-                gated = tile(f"o{c}_{b}", [P, PART], F32)
-                nc.vector.tensor_tensor(gated[:], gates[b][:].indirect(part_list(idx, c)), y[:, b, :], MULT)
-                nc.sync.dma_start(out=out[b * P : (b + 1) * P, c * PART : (c + 1) * PART], in_=gated[:])
-
-        for i in range(2):
-            for c in range(PARTS):
-                pick(i, c)
-        woven, ya, h, y = {}, {}, {}, {}
-        for step in range(PARTS + 4):
-            if step < PARTS:
-                pick(2, step)
-                pick(3, step)
-                woven[step] = weave(step)
-            if 0 <= step - 1 < PARTS:
-                ya[step - 1] = first_stage(step - 1, woven[step - 1])
-            if 0 <= step - 2 < PARTS:
-                h[step - 2] = join(step - 2, ya[step - 2])
-            if 0 <= step - 3 < PARTS:
-                y[step - 3] = second_stage(step - 3, h[step - 3])
-            if 0 <= step - 4 < PARTS:
-                gate_and_store(step - 4, y[step - 4])
+                gated = tile(f"o{j0}_{b}", [P, width], F32)
+                nc.vector.tensor_tensor(gated[:], gates[b][:].indirect(entries(idx, j0, width)), y[:, b, j0 : j0 + width], MULT)
+                nc.sync.dma_start(out=out[b * P : (b + 1) * P, j0 : j0 + width], in_=gated[:])
+            j0 = j0 + width

@@ -1,6 +1,7 @@
 from contextlib import ExitStack
 
 import concourse.mybir as mybir
+from concourse.masks import make_identity
 
 K, L, R, N, T, J = 512, 512, 512, 512, 2048, 1024
 FLOPS = 2 * J * (K * R + L * R + R * N)
@@ -18,23 +19,28 @@ MAX = mybir.AluOpType.max
 
 P = 128
 PACK = 4
-STRIPE = 16
-PART = 128
-PARTS = J // PART
-LOOKUP = 1024
-GATE = (256, 256, 256, 256)
-STEPS = (128, 128, 128, 128, 256, 256)
-LAST_PICKS = (512, 512)
-DIRECT = 4
+GROUP = 16
+QUADRANTS = 4
+BANK_J = 128
+OUT_BLOCKS = N // P
+WGT_BLOCKS = J // P
+WGT_ROWS = 2
+WGT_COPIES = GROUP // WGT_ROWS
+
+STEPS = (BANK_J,) * 4 + (2 * BANK_J,) * 2
+PSUM_MAX_STEPS = 4
+LAST_PICK = J // 2
+GATE_J = 256
+FIRST_BANKS = 5
 
 
-def load_scale_rows(queue, plane, rows):
-    for q in range(4):
-        queue.dma_start(out=plane[32 * q : 32 * q + 4, :].bitcast(I32), in_=rows[0, 4 * q : 4 * q + 4, :].bitcast(I32))
+def load_scale_rows(nc, plane, rows):
+    for q in range(QUADRANTS):
+        nc.sync.dma_start(out=plane[32 * q : 32 * q + 4, :].bitcast(I32), in_=rows[0, 4 * q : 4 * q + 4, :].bitcast(I32))
 
 
-def entries(offsets, j0, width):
-    return offsets[:, j0 // STRIPE : (j0 + width) // STRIPE]
+def entries(offsets, j0, count):
+    return offsets[:, j0 // GROUP : (j0 + count) // GROUP]
 
 
 def tile_list_htabg_max_gateL_kernel(
@@ -44,14 +50,14 @@ def tile_list_htabg_max_gateL_kernel(
     with ExitStack() as ctx:
         lists = ctx.enter_context(tc.tile_pool(name="lists", bufs=1))
         keep = ctx.enter_context(tc.tile_pool(name="keep", bufs=1))
-        psum1 = ctx.enter_context(tc.psum_pool(name="psum1", bufs=5))
-        psum2 = ctx.enter_context(tc.psum_pool(name="psum2", bufs=3))
+        psum1 = ctx.enter_context(tc.psum_pool(name="psum1", bufs=FIRST_BANKS))
+        psum2 = ctx.enter_context(tc.psum_pool(name="psum2", bufs=8 - FIRST_BANKS))
 
         def tile(name, shape, dtype):
             return keep.tile(shape, dtype, name=name, align_bytes=64)
 
-        idx = lists.tile([P, J // STRIPE], U16, name="idx")
-        idx2 = lists.tile([P, J // STRIPE], U16, name="idx2")
+        idx = lists.tile([P, J // GROUP], U16, name="idx")
+        idx2 = lists.tile([P, J // GROUP], U16, name="idx2")
 
         tab_s = tile("tab_s", [P, T], U8)
         wa_s_raw = tile("wa_s_raw", [P, R], U8)
@@ -63,29 +69,48 @@ def tile_list_htabg_max_gateL_kernel(
         wb_raw = tile("wb_raw", [P, PACK, R], F32)
         tab_w = tile("tab_w", [P, T], I32)
         wgt = tile("wgt", [P, J], F32)
+        wgt_rows = tile("wgt_rows", [P, P], F32)
         wd_w = tile("wd_w", [P, 2 * N], U8)
         x_rows = xT.rearrange("(p i) t -> p i t", i=PACK)
         x_planes = [tile(f"x{i}", [P, T], F32) for i in range(PACK)]
-        gates = [tile(f"g{b}", [P, T], F32) for b in range(N // P)]
+        gates = [tile(f"g{b}", [P, T], F32) for b in range(OUT_BLOCKS)]
 
-        nc.sync.dma_start(idx[:], offs)
-        nc.sync.dma_start(out=tab_w[:], in_=tab_words[0].rearrange("p t i -> p (t i)").bitcast(I32))
-        load_scale_rows(nc.sync, tab_s, tab_scales)
-        nc.sync.dma_start(idx2[:], offs2)
-        nc.sync.dma_start(out=wb_raw[:], in_=wb.rearrange("(p i) r -> p i r", i=PACK))
+        nc.sync.dma_start(
+            out=wgt_rows[:],
+            in_=wgt2.rearrange("(g s) j -> g (s j)", s=GROUP)[:, 0 : WGT_ROWS * J].rearrange("g (r c) -> g r c", c=P),
+        )
         nc.sync.dma_start(out=wa_w_raw[:], in_=wa_words[0].rearrange("p r i -> p (r i)").bitcast(I32))
-        load_scale_rows(nc.sync, wa_s_raw, wa_scales)
-        nc.sync.dma_start(out=wgt[:], in_=wgt2)
-        nc.sync.dma_start(out=x_planes[0][:], in_=x_rows[:, 0, :])
-        nc.sync.dma_start(out=x_planes[1][:], in_=x_rows[:, 1, :])
-        load_scale_rows(nc.sync, wd_s, wd_scales)
-        nc.sync.dma_start(out=x_planes[2][:], in_=x_rows[:, 2, :])
-        nc.sync.dma_start(out=x_planes[3][:], in_=x_rows[:, 3, :])
+        nc.sync.dma_start(idx[:], offs)
+        load_scale_rows(nc, tab_s, tab_scales)
+        nc.sync.dma_start(out=tab_w[:], in_=tab_words[0].rearrange("p t i -> p (t i)").bitcast(I32))
+        nc.sync.dma_start(out=wb_raw[:], in_=wb.rearrange("(p i) r -> p i r", i=PACK))
+        load_scale_rows(nc, wa_s_raw, wa_scales)
+        nc.sync.dma_start(idx2[:], offs2)
+        for i in range(PACK):
+            if i == PACK // 2:
+                load_scale_rows(nc, wd_s, wd_scales)
+            nc.sync.dma_start(out=x_planes[i][:], in_=x_rows[:, i, :])
         nc.sync.dma_start(out=wd_w[:].bitcast(I32), in_=wd_words[0].bitcast(I32))
-        nc.sync.dma_start(out=gates[0][:], in_=gT[0 * P : 1 * P, :])
-        nc.sync.dma_start(out=gates[1][:], in_=gT[1 * P : 2 * P, :])
-        nc.sync.dma_start(out=gates[2][:], in_=gT[2 * P : 3 * P, :])
-        nc.sync.dma_start(out=gates[3][:], in_=gT[3 * P : 4 * P, :])
+        for b in range(OUT_BLOCKS):
+            nc.sync.dma_start(out=gates[b][:], in_=gT[b * P : (b + 1) * P, :])
+
+        identity = tile("identity", [P, P], F32)
+        make_identity(nc, identity[:])
+        turned = psum2.tile([P, OUT_BLOCKS, BANK_J], F32, name="second")
+        nc.tensor.transpose(turned[:, 0, :], wgt_rows[:], identity[:])
+        spread = tile("spread", [P, WGT_BLOCKS, P // WGT_COPIES, WGT_COPIES], F32)
+        nc.scalar.copy(
+            out=spread[:],
+            in_=turned[:, 0, :]
+            .rearrange("c (row u) -> c u row", u=WGT_BLOCKS)
+            .unsqueeze(3)
+            .to_broadcast([P, WGT_BLOCKS, P // WGT_COPIES, WGT_COPIES]),
+        )
+        for u0 in range(0, WGT_BLOCKS, OUT_BLOCKS):
+            back = psum2.tile([P, OUT_BLOCKS, BANK_J], F32, name="second")
+            for u in range(OUT_BLOCKS):
+                nc.tensor.transpose(back[:, u, :], spread[:, u0 + u, :, :].rearrange("c row a -> c (row a)"), identity[:])
+            nc.scalar.copy(out=wgt[:, u0 * P : (u0 + OUT_BLOCKS) * P], in_=back[:].rearrange("p u c -> p (u c)"))
 
         v_s = tile("v_s", [P, J], U8)
         nc.vector.tensor_copy(v_s[:], tab_s[:].indirect(idx[:]))
@@ -99,27 +124,34 @@ def tile_list_htabg_max_gateL_kernel(
             out=wa_s[:].rearrange("p (t m) -> p t m", t=PACK), in_=wa_s_raw[:].rearrange("p (m t) -> p t m", t=PACK)
         )
 
-        wb_bf = tile("wb_bf", [P, PACK * R], BF16)
-        nc.scalar.copy(
-            out=wb_bf[:].rearrange("p (t m i) -> p m i t", t=PACK, i=PACK),
-            in_=wb_raw[:].rearrange("p i (m t) -> p m i t", t=PACK),
-        )
         wb_w = tile("wb_w", [P, R], U32)
         wb_s = tile("wb_s", [P, R], U8)
-        nc.vector.quantize_mx(out=wb_w[:].bitcast(FP8X4), scales=wb_s[:], in_=wb_bf[:])
+        for half, copy in enumerate((nc.scalar.copy, nc.vector.tensor_copy)):
+            wb_woven = tile(f"wb_bf{half}", [P, R // 2 * PACK], BF16)
+            copy(
+                out=wb_woven[:].rearrange("p (t m i) -> p m i t", t=2, i=PACK),
+                in_=wb_raw[:].rearrange("p i (m t) -> p m i t", t=PACK)[:, :, :, 2 * half : 2 * half + 2],
+            )
+            dealt = slice(half * R // 2, (half + 1) * R // 2)
+            nc.vector.quantize_mx(out=wb_w[:, dealt].bitcast(FP8X4), scales=wb_s[:, dealt], in_=wb_woven[:])
 
-        picked = tile("picked", [P, PACK, J], F32)
+        xg = tile("picked", [P, PACK, J], F32)
+
+        def pick(i, j0, count):
+            cols = slice(j0, j0 + count)
+            nc.vector.tensor_tensor(xg[:, i, cols], x_planes[i][:].indirect(entries(idx2, j0, count)), wgt[:, cols], MULT)
+
         for i in range(PACK - 1):
-            nc.vector.tensor_tensor(picked[:, i, :], x_planes[i][:].indirect(idx2[:]), wgt[:], MULT)
+            pick(i, 0, J)
 
-        def project(w_words, w_scales, words, scales):
-            bank = psum1.tile([P, PACK, PART], F32, name="first")
+        def first_layer(w_words, w_scales, words, scales):
+            bank = psum1.tile([P, PACK, BANK_J], F32, name="first")
             for t in range(PACK):
-                rows = slice(t * P, (t + 1) * P)
+                dealt = slice(t * P, (t + 1) * P)
                 nc.tensor.matmul_mx(
                     out=bank[:, t, :],
-                    lhsT=w_words[:, rows].bitcast(FP8X4),
-                    lhsT_scale=w_scales[:, rows],
+                    lhsT=w_words[:, dealt].bitcast(FP8X4),
+                    lhsT_scale=w_scales[:, dealt],
                     rhs=words.bitcast(FP8X4),
                     rhs_scale=scales,
                     start=True,
@@ -127,78 +159,67 @@ def tile_list_htabg_max_gateL_kernel(
                 )
             return bank[:].rearrange("p t j -> p j t")
 
-
-        def quantise(name, values):
-            width = values.shape[1]
+        def quantise(name, woven):
+            width = woven.shape[1]
             words = tile(name + "_w", [P, width], U32)
             scales = tile(name + "_s", [P, width], U8)
             nc.vector.quantize_mx(
-                out=words[:].bitcast(FP8X4), scales=scales[:], in_=values[:].rearrange("p j t -> p (j t)")
+                out=words[:].bitcast(FP8X4), scales=scales[:], in_=woven[:].rearrange("p j t -> p (j t)")
             )
             return words, scales
 
         v_w = tile("v_w", [P, J], U32)
-        y = tile("y", [P, N // P, J], F32)
+        y = tile("y", [P, OUT_BLOCKS, J], F32)
         yb = tile("yb", [P, J, PACK], BF16)
+        nc.vector.tensor_copy(v_w[:], tab_w[:].bitcast(U32).indirect(idx[:]))
+        for j0 in range(0, J, BANK_J):
+            cols = slice(j0, j0 + BANK_J)
+            nc.scalar.copy(out=yb[:, cols, :], in_=first_layer(wb_w, wb_s, v_w[:, cols], v_s[:, cols]))
 
-        def look_up(c):
-            cols = slice(c * PART, (c + 1) * PART)
-            if c * PART % LOOKUP == 0:
-                nc.vector.tensor_copy(
-                    v_w[:, c * PART : c * PART + LOOKUP], tab_w[:].bitcast(U32).indirect(entries(idx, c * PART, LOOKUP))
-                )
-            nc.scalar.copy(out=yb[:, cols, :], in_=project(wb_w, wb_s, v_w[:, cols], v_s[:, cols]))
-
-        for c in range(PARTS):
-            look_up(c)
-
-        pick_starts = [sum(LAST_PICKS[:n]) for n in range(len(LAST_PICKS))]
         j0 = 0
-        for c, width in enumerate(STEPS):
-            for start, count in zip(pick_starts, LAST_PICKS):
-                if j0 <= start < j0 + width:
-                    wide = slice(start, start + count)
-                    nc.vector.tensor_tensor(
-                        picked[:, PACK - 1, wide], x_planes[PACK - 1][:].indirect(entries(idx2, start, count)), wgt[:, wide], MULT
-                    )
-            woven = tile(f"xb{c}", [P, width, PACK], BF16)
+        for step, width in enumerate(STEPS):
+            if j0 % LAST_PICK == 0:
+                pick(PACK - 1, j0, LAST_PICK)
+            banks = [slice(u, u + BANK_J) for u in range(0, width, BANK_J)]
+
+            x_woven = tile(f"xb{step}", [P, width, PACK], BF16)
             nc.scalar.copy(
-                out=woven[:].rearrange("p (u v) i -> p u i v", v=4),
-                in_=picked[:, :, j0 : j0 + width].rearrange("p i (u v) -> p u i v", v=4),
+                out=x_woven[:].rearrange("p (u v) i -> p u i v", v=4),
+                in_=xg[:, :, j0 : j0 + width].rearrange("p i (u v) -> p u i v", v=4),
             )
-            x_w, x_s = quantise(f"xq{c}", woven)
-            h = tile(f"h{c}", [P, width, PACK], BF16)
-            if c < DIRECT:
-                for u in range(0, width, PART):
-                    ya = project(wa_w, wa_s, x_w[:, u : u + PART], x_s[:, u : u + PART])
-                    nc.vector.tensor_tensor(h[:, u : u + PART, :], ya, yb[:, j0 + u : j0 + u + PART, :], MAX)
+            x_w, x_s = quantise(f"xq{step}", x_woven)
+
+            h = tile(f"h{step}", [P, width, PACK], BF16)
+            yb_step = yb[:, j0 : j0 + width, :]
+            if step < PSUM_MAX_STEPS:
+                for cols in banks:
+                    ya_sums = first_layer(wa_w, wa_s, x_w[:, cols], x_s[:, cols])
+                    nc.vector.tensor_tensor(h[:, cols, :], ya_sums, yb_step[:, cols, :], MAX)
             else:
-                ya = tile(f"ya{c}", [P, width, PACK], BF16)
-                for u in range(0, width, PART):
-                    nc.scalar.copy(
-                        out=ya[:, u : u + PART, :], in_=project(wa_w, wa_s, x_w[:, u : u + PART], x_s[:, u : u + PART])
-                    )
-                nc.vector.tensor_tensor(h[:], ya[:], yb[:, j0 : j0 + width, :], MAX)
-            h_w, h_s = quantise(f"hq{c}", h)
-            for u in range(0, width, PART):
-                bank = psum2.tile([P, N // P, PART], F32, name="second")
-                for b in range(N // P):
+                ya = tile(f"ya{step}", [P, width, PACK], BF16)
+                for cols in banks:
+                    nc.scalar.copy(out=ya[:, cols, :], in_=first_layer(wa_w, wa_s, x_w[:, cols], x_s[:, cols]))
+                nc.vector.tensor_tensor(h[:], ya[:], yb_step, MAX)
+            h_w, h_s = quantise(f"hq{step}", h)
+
+            for cols in banks:
+                bank = psum2.tile([P, OUT_BLOCKS, BANK_J], F32, name="second")
+                for b in range(OUT_BLOCKS):
                     nc.tensor.matmul_mx(
                         out=bank[:, b, :],
                         lhsT=wd_w[:, 2 * b * P : 2 * (b + 1) * P].bitcast(FP4X4),
                         lhsT_scale=wd_s[:, b * P : (b + 1) * P],
-                        rhs=h_w[:, u : u + PART].bitcast(FP8X4),
-                        rhs_scale=h_s[:, u : u + PART],
+                        rhs=h_w[:, cols].bitcast(FP8X4),
+                        rhs_scale=h_s[:, cols],
                         start=True,
                         stop=True,
                     )
-                nc.scalar.copy(out=y[:, :, j0 + u : j0 + u + PART], in_=bank[:])
+                nc.scalar.copy(out=y[:, :, j0 : j0 + width][:, :, cols], in_=bank[:])
             j0 = j0 + width
 
-        j0 = 0
-        for width in GATE:
-            for b in range(N // P):
-                gated = tile(f"o{j0}_{b}", [P, width], F32)
-                nc.vector.tensor_tensor(gated[:], gates[b][:].indirect(entries(idx, j0, width)), y[:, b, j0 : j0 + width], MULT)
-                nc.sync.dma_start(out=out[b * P : (b + 1) * P, j0 : j0 + width], in_=gated[:])
-            j0 = j0 + width
+        for j0 in range(0, J, GATE_J):
+            cols = slice(j0, j0 + GATE_J)
+            for b in range(OUT_BLOCKS):
+                gated = tile(f"o{j0}_{b}", [P, GATE_J], F32)
+                nc.vector.tensor_tensor(gated[:], gates[b][:].indirect(entries(idx, j0, GATE_J)), y[:, b, cols], MULT)
+                nc.sync.dma_start(out=out[b * P : (b + 1) * P, cols], in_=gated[:])

@@ -83,10 +83,11 @@ def tile_list_htabg_max_gateL_kernel(
         nc.sync.dma_start(idx[:], offs)
         load_scale_rows(nc, tab_s, tab_scales)
         nc.sync.dma_start(out=tab_w[:], in_=tab_words[0].rearrange("p t i -> p (t i)").bitcast(I32))
-        nc.sync.dma_start(out=wb_raw[:], in_=wb.rearrange("(p i) r -> p i r", i=PACK))
         load_scale_rows(nc, wa_s_raw, wa_scales)
         nc.sync.dma_start(idx2[:], offs2)
-        for i in range(PACK):
+        nc.sync.dma_start(out=x_planes[0][:], in_=x_rows[:, 0, :])
+        nc.sync.dma_start(out=wb_raw[:], in_=wb.rearrange("(p i) r -> p i r", i=PACK))
+        for i in range(1, PACK):
             if i == PACK // 2:
                 load_scale_rows(nc, wd_s, wd_scales)
             nc.sync.dma_start(out=x_planes[i][:], in_=x_rows[:, i, :])

@@ -27,11 +27,27 @@ WGT_BLOCKS = J // P
 WGT_ROWS = 2
 WGT_COPIES = GROUP // WGT_ROWS
 
-STEPS = (BANK_J,) * 4 + (2 * BANK_J,) * 2
+
+ORDER = ["wgt","wa","idx","tab_s","tab","wa_s","idx2","x0","wb","x1","wd_s","x2","x3","wd","g0","g1","g2","g3"]
+STEPS = [128,128,128,128,256,256]
 PSUM_MAX_STEPS = 4
-LAST_PICK = J // 2
-GATE_J = 256
-FIRST_BANKS = 5
+PRE_WEAVE = False
+WB_VECTOR = 2
+PIECES = [1024]
+WORDS = [1024]
+WORDS_IN_LOOP = False
+GATE_J = [512,512]
+LAG_A = 1
+LAG_Y = 2
+PLAN = [["d",0,0],["d",1,0],["w",0,0],["b",0,0],["b",128,0],["b",256,0],["b",384,0],["b",512,0],["b",640,0],["b",768,0],["b",896,0],["p",0,0],["p",1,0],["p",2,0],["p",3,0],["x",0,0],["x",1,0],["h",0,0],["p",3,256],["x",2,0],["h",1,0],["y",0,0],["x",3,0],["h",2,0],["y",1,0],["p",3,512],["x",4,0],["h",3,0],["y",2,0],["p",3,768],["x",5,0],["h",4,0],["y",3,0],["h",5,0],["y",4,0],["y",5,0],["g",0,0],["g",0,1],["g",0,2],["g",256,0],["g",256,1],["g",256,2],["g",0,3],["g",512,0],["g",512,1],["g",512,2],["g",512,3],["g",768,0],["g",768,1]]
+TAB_A = 512
+TAGS = {}
+HOLD = {0: 768}
+LAST = [256,256,256,256]
+PRE_STEPS = []
+GATE_W = {(0, 3): 512, (512, 2): 512, (512, 3): 512}
+BANKS = 8
+PROBES = []
 
 
 def load_scale_rows(nc, plane, rows):
@@ -43,6 +59,15 @@ def entries(offsets, j0, count):
     return offsets[:, j0 // GROUP : (j0 + count) // GROUP]
 
 
+def starts(widths):
+    return {sum(widths[:n]): w for n, w in enumerate(widths)}
+
+
+def within(parts, j0):
+    p0 = max(p for p in parts if p <= j0)
+    return parts[p0], j0 - p0
+
+
 def tile_list_htabg_max_gateL_kernel(
     tc, tab_words, tab_scales, xT, wgt2, wa_words, wa_scales, wb, wd_words, wd_scales, gT, offs, offs2, out
 ):
@@ -50,11 +75,20 @@ def tile_list_htabg_max_gateL_kernel(
     with ExitStack() as ctx:
         lists = ctx.enter_context(tc.tile_pool(name="lists", bufs=1))
         keep = ctx.enter_context(tc.tile_pool(name="keep", bufs=1))
-        psum1 = ctx.enter_context(tc.psum_pool(name="psum1", bufs=FIRST_BANKS))
-        psum2 = ctx.enter_context(tc.psum_pool(name="psum2", bufs=8 - FIRST_BANKS))
+        psum = ctx.enter_context(tc.psum_pool(name="psum", bufs=1))
+        used = []
 
-        def tile(name, shape, dtype):
-            return keep.tile(shape, dtype, name=name, align_bytes=64)
+        def tile(name, shape, dtype, tag=None):
+            return keep.tile(shape, dtype, name=name, tag=TAGS.get(name, tag or name), align_bytes=64)
+
+        def next_bank():
+            used.append(len(used))
+            return psum.tile([P, PACK, BANK_J], F32, name=f"bank{len(used) % BANKS}")
+
+        def probe(name, ap):
+            if name in PROBES:
+                clock = tile("clock_" + name, [P, 1], ap.dtype)
+                nc.gpsimd.tensor_copy(out=clock[:], in_=ap)
 
         idx = lists.tile([P, J // GROUP], U16, name="idx")
         idx2 = lists.tile([P, J // GROUP], U16, name="idx2")
@@ -75,29 +109,38 @@ def tile_list_htabg_max_gateL_kernel(
         x_planes = [tile(f"x{i}", [P, T], F32) for i in range(PACK)]
         gates = [tile(f"g{b}", [P, T], F32) for b in range(OUT_BLOCKS)]
 
-        nc.sync.dma_start(
-            out=wgt_rows[:],
-            in_=wgt2.rearrange("(g s) j -> g (s j)", s=GROUP)[:, 0 : WGT_ROWS * J].rearrange("g (r c) -> g r c", c=P),
-        )
-        nc.sync.dma_start(out=wa_w_raw[:], in_=wa_words[0].rearrange("p r i -> p (r i)").bitcast(I32))
-        nc.sync.dma_start(idx[:], offs)
-        load_scale_rows(nc, tab_s, tab_scales)
-        nc.sync.dma_start(out=tab_w[:], in_=tab_words[0].rearrange("p t i -> p (t i)").bitcast(I32))
-        load_scale_rows(nc, wa_s_raw, wa_scales)
-        nc.sync.dma_start(idx2[:], offs2)
-        nc.sync.dma_start(out=x_planes[0][:], in_=x_rows[:, 0, :])
-        nc.sync.dma_start(out=wb_raw[:], in_=wb.rearrange("(p i) r -> p i r", i=PACK))
-        for i in range(1, PACK):
-            if i == PACK // 2:
-                load_scale_rows(nc, wd_s, wd_scales)
-            nc.sync.dma_start(out=x_planes[i][:], in_=x_rows[:, i, :])
-        nc.sync.dma_start(out=wd_w[:].bitcast(I32), in_=wd_words[0].bitcast(I32))
-        for b in range(OUT_BLOCKS):
-            nc.sync.dma_start(out=gates[b][:], in_=gT[b * P : (b + 1) * P, :])
+        tab_rows = tab_words[0].rearrange("p t i -> p (t i)").bitcast(I32)
+        loads = {
+            "wgt": lambda: nc.sync.dma_start(
+                out=wgt_rows[:],
+                in_=wgt2.rearrange("(e s) j -> e s j", s=WGT_COPIES)[:, 0, :].rearrange("e (u c) -> e u c", c=P),
+            ),
+            "wa": lambda: nc.sync.dma_start(out=wa_w_raw[:], in_=wa_words[0].rearrange("p r i -> p (r i)").bitcast(I32)),
+            "idx": lambda: nc.sync.dma_start(idx[:], offs),
+            "idx2": lambda: nc.sync.dma_start(idx2[:], offs2),
+            "tab_s": lambda: load_scale_rows(nc, tab_s, tab_scales),
+            "wa_s": lambda: load_scale_rows(nc, wa_s_raw, wa_scales),
+            "wd_s": lambda: load_scale_rows(nc, wd_s, wd_scales),
+            "tab": lambda: nc.sync.dma_start(out=tab_w[:], in_=tab_words[0].rearrange("p t i -> p (t i)").bitcast(I32)),
+            "tabA": lambda: nc.sync.dma_start(out=tab_w[:, 0:TAB_A], in_=tab_rows[:, 0:TAB_A]),
+            "tabB": lambda: nc.sync.dma_start(out=tab_w[:, TAB_A:T], in_=tab_rows[:, TAB_A:T]),
+            "wb": lambda: nc.sync.dma_start(out=wb_raw[:], in_=wb.rearrange("(p i) r -> p i r", i=PACK)),
+            "wd": lambda: nc.sync.dma_start(out=wd_w[:].bitcast(I32), in_=wd_words[0].bitcast(I32)),
+        }
+        for name in ORDER:
+            if name[0] == "x":
+                nc.sync.dma_start(out=x_planes[int(name[1])][:], in_=x_rows[:, int(name[1]), :])
+            elif name[0] == "g":
+                b = int(name[1])
+                nc.sync.dma_start(out=gates[b][:], in_=gT[b * P : (b + 1) * P, :])
+            else:
+                loads[name]()
 
+        probe("x3", x_planes[3][:, 0:1])
+        probe("x1", x_planes[1][:, 0:1])
         identity = tile("identity", [P, P], F32)
         make_identity(nc, identity[:])
-        turned = psum2.tile([P, OUT_BLOCKS, BANK_J], F32, name="second")
+        turned = next_bank()
         nc.tensor.transpose(turned[:, 0, :], wgt_rows[:], identity[:])
         spread = tile("spread", [P, WGT_BLOCKS, P // WGT_COPIES, WGT_COPIES], F32)
         nc.scalar.copy(
@@ -108,56 +151,46 @@ def tile_list_htabg_max_gateL_kernel(
             .to_broadcast([P, WGT_BLOCKS, P // WGT_COPIES, WGT_COPIES]),
         )
         for u0 in range(0, WGT_BLOCKS, OUT_BLOCKS):
-            back = psum2.tile([P, OUT_BLOCKS, BANK_J], F32, name="second")
+            back = next_bank()
             for u in range(OUT_BLOCKS):
                 nc.tensor.transpose(back[:, u, :], spread[:, u0 + u, :, :].rearrange("c row a -> c (row a)"), identity[:])
             nc.scalar.copy(out=wgt[:, u0 * P : (u0 + OUT_BLOCKS) * P], in_=back[:].rearrange("p u c -> p (u c)"))
+        probe("wgt", wgt[:, J - 1 : J])
 
         v_s = tile("v_s", [P, J], U8)
         nc.vector.tensor_copy(v_s[:], tab_s[:].indirect(idx[:]))
-
-        wa_w = tile("wa_w", [P, R], I32)
-        nc.vector.tensor_copy(
-            out=wa_w[:].rearrange("p (t m) -> p t m", t=PACK), in_=wa_w_raw[:].rearrange("p (m t) -> p t m", t=PACK)
-        )
-        wa_s = tile("wa_s", [P, R], U8)
-        nc.vector.tensor_copy(
-            out=wa_s[:].rearrange("p (t m) -> p t m", t=PACK), in_=wa_s_raw[:].rearrange("p (m t) -> p t m", t=PACK)
-        )
+        probe("v_s", v_s[:, J - 4 : J].bitcast(I32))
 
         wb_w = tile("wb_w", [P, R], U32)
         wb_s = tile("wb_s", [P, R], U8)
-        for half, copy in enumerate((nc.scalar.copy, nc.vector.tensor_copy)):
-            wb_woven = tile(f"wb_bf{half}", [P, R // 2 * PACK], BF16)
+        for half in range(2):
+            on_vector = half * 2 >= PACK - WB_VECTOR
+            copy = nc.vector.tensor_copy if on_vector else nc.scalar.copy
+            wb_woven = tile(f"wb_bf{half}", [P, R // 2 * PACK], BF16, tag=None if half else "spread")
             copy(
                 out=wb_woven[:].rearrange("p (t m i) -> p m i t", t=2, i=PACK),
                 in_=wb_raw[:].rearrange("p i (m t) -> p m i t", t=PACK)[:, :, :, 2 * half : 2 * half + 2],
             )
             dealt = slice(half * R // 2, (half + 1) * R // 2)
             nc.vector.quantize_mx(out=wb_w[:, dealt].bitcast(FP8X4), scales=wb_s[:, dealt], in_=wb_woven[:])
+        probe("wb_w", wb_w[:, R - 1 : R])
 
-        xg = tile("picked", [P, PACK, J], F32)
-
-        def pick(i, j0, count):
-            cols = slice(j0, j0 + count)
-            nc.vector.tensor_tensor(xg[:, i, cols], x_planes[i][:].indirect(entries(idx2, j0, count)), wgt[:, cols], MULT)
-
-        for i in range(PACK - 1):
-            pick(i, 0, J)
-
-        def first_layer(w_words, w_scales, words, scales):
-            bank = psum1.tile([P, PACK, BANK_J], F32, name="first")
+        def product(w_words, w_scales, words, scales):
+            bank = next_bank()
             for t in range(PACK):
-                dealt = slice(t * P, (t + 1) * P)
                 nc.tensor.matmul_mx(
                     out=bank[:, t, :],
-                    lhsT=w_words[:, dealt].bitcast(FP8X4),
-                    lhsT_scale=w_scales[:, dealt],
+                    lhsT=w_words(t),
+                    lhsT_scale=w_scales[:, t * P : (t + 1) * P],
                     rhs=words.bitcast(FP8X4),
                     rhs_scale=scales,
                     start=True,
                     stop=True,
                 )
+            return bank
+
+        def first_layer(w_words, w_scales, words, scales):
+            bank = product(lambda t: w_words[:, t * P : (t + 1) * P].bitcast(FP8X4), w_scales, words, scales)
             return bank[:].rearrange("p t j -> p j t")
 
         def quantise(name, woven):
@@ -169,58 +202,116 @@ def tile_list_htabg_max_gateL_kernel(
             )
             return words, scales
 
-        v_w = tile("v_w", [P, J], U32)
-        y = tile("y", [P, OUT_BLOCKS, J], F32)
-        yb = tile("yb", [P, J, PACK], BF16)
-        nc.vector.tensor_copy(v_w[:], tab_w[:].bitcast(U32).indirect(idx[:]))
-        for j0 in range(0, J, BANK_J):
-            cols = slice(j0, j0 + BANK_J)
-            nc.scalar.copy(out=yb[:, cols, :], in_=first_layer(wb_w, wb_s, v_w[:, cols], v_s[:, cols]))
+        y = {j0: tile(f"y{j0}", [P, OUT_BLOCKS, count], F32) for j0, count in starts(GATE_J).items()}
+        yb = {j0: tile(f"yb{j0}", [P, width, PACK], BF16) for j0, width in starts(STEPS).items()}
+        v_pieces = {}
 
-        j0 = 0
-        for step, width in enumerate(STEPS):
-            if j0 % LAST_PICK == 0:
-                pick(PACK - 1, j0, LAST_PICK)
-            banks = [slice(u, u + BANK_J) for u in range(0, width, BANK_J)]
+        def look_up(j0, count):
+            v_pieces[j0] = tile(f"v_w{j0}", [P, count], U32)
+            nc.vector.tensor_copy(v_pieces[j0][:], tab_w[:].bitcast(U32).indirect(entries(idx, j0, count)))
 
-            x_woven = tile(f"xb{step}", [P, width, PACK], BF16)
-            nc.scalar.copy(
-                out=x_woven[:].rearrange("p (u v) i -> p u i v", v=4),
-                in_=xg[:, :, j0 : j0 + width].rearrange("p i (u v) -> p u i v", v=4),
+        def make_yb(j0):
+            into, at = within(yb, j0)
+            words, w0 = within(v_pieces, j0)
+            sums = first_layer(wb_w, wb_s, words[:, w0 : w0 + BANK_J], v_s[:, j0 : j0 + BANK_J])
+            nc.scalar.copy(out=into[:, at : at + BANK_J, :], in_=sums)
+
+        pieces = starts(PIECES)
+        xg = {j0: tile(f"picked{j0}", [P, PACK * count], F32)[:].rearrange("p (i j) -> p i j", i=PACK) for j0, count in pieces.items()}
+
+        def pick(i, j0, count):
+            nc.vector.tensor_tensor(
+                within(xg, j0)[0][:, i, within(xg, j0)[1] : within(xg, j0)[1] + count], x_planes[i][:].indirect(entries(idx2, j0, count)), wgt[:, j0 : j0 + count], MULT
             )
-            x_w, x_s = quantise(f"xq{step}", x_woven)
 
+        steps = list(starts(STEPS).items())
+        x_woven = {}
+
+        def woven_tile(step):
+            width = STEPS[step]
+            if step not in x_woven:
+                if step in HOLD:
+                    held, at = within(xg, HOLD[step])
+                    room = held[:, PACK - 1, at : at + 2 * width].bitcast(BF16)
+                else:
+                    room = tile(f"xb{step}", [P, width * PACK], BF16)[:]
+                x_woven[step] = room.rearrange("p (j i) -> p j i", i=PACK)
+            return x_woven[step]
+
+        def weave(step, i0, i1):
+            j0, width = steps[step]
+            source, at = within(xg, j0)
+            nc.scalar.copy(
+                out=woven_tile(step)[:, :, i0:i1].rearrange("p (u v) i -> p u i v", v=4),
+                in_=source[:, i0:i1, at : at + width].rearrange("p i (u v) -> p u i v", v=4),
+            )
+
+        wa_w = tile("wa_w", [P, R], I32)
+        wa_s = tile("wa_s", [P, R], U8)
+
+        def deal(which):
+            into, raw = ((wa_w, wa_w_raw), (wa_s, wa_s_raw))[which]
+            (nc.vector, nc.gpsimd)[which].tensor_copy(out=into[:].rearrange("p (t m) -> p t m", t=PACK), in_=raw[:].rearrange("p (m t) -> p t m", t=PACK))
+
+        x_q = {}
+        h_q = {}
+
+        def stage_x(step):
+            j0, width = steps[step]
+            weave(step, 2 if step in PRE_STEPS else 0, PACK)
+            x_q[step] = quantise(f"xq{step}", x_woven[step])
+            probe(f"xq{step}", x_q[step][0][:, 0:1])
+
+        def stage_h(step):
+            j0, width = steps[step]
+            x_w, x_s = x_q[step]
+            banks = [slice(u, u + BANK_J) for u in range(0, width, BANK_J)]
             h = tile(f"h{step}", [P, width, PACK], BF16)
-            yb_step = yb[:, j0 : j0 + width, :]
             if step < PSUM_MAX_STEPS:
                 for cols in banks:
                     ya_sums = first_layer(wa_w, wa_s, x_w[:, cols], x_s[:, cols])
-                    nc.vector.tensor_tensor(h[:, cols, :], ya_sums, yb_step[:, cols, :], MAX)
+                    nc.vector.tensor_tensor(h[:, cols, :], ya_sums, yb[j0][:, cols, :], MAX)
             else:
                 ya = tile(f"ya{step}", [P, width, PACK], BF16)
                 for cols in banks:
                     nc.scalar.copy(out=ya[:, cols, :], in_=first_layer(wa_w, wa_s, x_w[:, cols], x_s[:, cols]))
-                nc.vector.tensor_tensor(h[:], ya[:], yb_step, MAX)
-            h_w, h_s = quantise(f"hq{step}", h)
+                nc.vector.tensor_tensor(h[:], ya[:], yb[j0][:], MAX)
+            h_q[step] = quantise(f"hq{step}", h)
 
-            for cols in banks:
-                bank = psum2.tile([P, OUT_BLOCKS, BANK_J], F32, name="second")
-                for b in range(OUT_BLOCKS):
-                    nc.tensor.matmul_mx(
-                        out=bank[:, b, :],
-                        lhsT=wd_w[:, 2 * b * P : 2 * (b + 1) * P].bitcast(FP4X4),
-                        lhsT_scale=wd_s[:, b * P : (b + 1) * P],
-                        rhs=h_w[:, cols].bitcast(FP8X4),
-                        rhs_scale=h_s[:, cols],
-                        start=True,
-                        stop=True,
-                    )
-                nc.scalar.copy(out=y[:, :, j0 : j0 + width][:, :, cols], in_=bank[:])
-            j0 = j0 + width
+        def stage_y(step):
+            j0, width = steps[step]
+            h_w, h_s = h_q[step]
+            for u in range(0, width, BANK_J):
+                cols = slice(u, u + BANK_J)
+                bank = product(lambda b: wd_w[:, 2 * b * P : 2 * (b + 1) * P].bitcast(FP4X4), wd_s, h_w[:, cols], h_s[:, cols])
+                into, at = within(y, j0 + u)
+                nc.scalar.copy(out=into[:, :, at : at + BANK_J], in_=bank[:])
+            probe(f"y{step}", into[:, 0, at : at + 1])
 
-        for j0 in range(0, J, GATE_J):
-            cols = slice(j0, j0 + GATE_J)
-            for b in range(OUT_BLOCKS):
-                gated = tile(f"o{j0}_{b}", [P, GATE_J], F32)
-                nc.vector.tensor_tensor(gated[:], gates[b][:].indirect(entries(idx, j0, GATE_J)), y[:, b, cols], MULT)
-                nc.sync.dma_start(out=out[b * P : (b + 1) * P, cols], in_=gated[:])
+        def gate(j0, b):
+            count = GATE_W.get((j0, b), 256)
+            sums, at = within(y, j0)
+            gated = tile(f"o{j0}_{b}", [P, count], F32)
+            nc.vector.tensor_tensor(gated[:], gates[b][:].indirect(entries(idx, j0, count)), sums[:, b, at : at + count], MULT)
+            nc.sync.dma_start(out=out[b * P : (b + 1) * P, j0 : j0 + count], in_=gated[:])
+
+        for what, a, b in PLAN:
+            if what == "p":
+                pick(a, b, pieces[b] if a < PACK - 1 else starts(LAST)[b])
+                probe(f"p{a}_{b}", within(xg, b)[0][:, a, within(xg, b)[1] : within(xg, b)[1] + 1])
+            elif what == "w":
+                look_up(a, starts(WORDS)[a])
+            elif what == "d":
+                deal(a)
+            elif what == "x":
+                stage_x(a)
+            elif what == "h":
+                stage_h(a)
+            elif what == "y":
+                stage_y(a)
+            elif what == "b":
+                make_yb(a)
+            elif what == "e":
+                weave(a, 0, 2)
+            else:
+                gate(a, b)

@@ -21,33 +21,16 @@ P = 128
 PACK = 4
 GROUP = 16
 QUADRANTS = 4
+BANKS = 8
 BANK_J = 128
 OUT_BLOCKS = N // P
 WGT_BLOCKS = J // P
-WGT_ROWS = 2
-WGT_COPIES = GROUP // WGT_ROWS
+WGT_COPIES = 8
+HALF, QUARTER = J // 2, J // 4
 
-
-ORDER = ["wgt","wa","idx","tab_s","tab","wa_s","idx2","x0","wb","x1","wd_s","x2","x3","wd","g0","g1","g2","g3"]
-STEPS = [128,128,128,128,256,256]
+STEPS = (BANK_J,) * 4 + (2 * BANK_J,) * 2
 PSUM_MAX_STEPS = 4
-PRE_WEAVE = False
-WB_VECTOR = 2
-PIECES = [1024]
-WORDS = [1024]
-WORDS_IN_LOOP = False
-GATE_J = [512,512]
-LAG_A = 1
-LAG_Y = 2
-PLAN = [["d",0,0],["d",1,0],["w",0,0],["b",0,0],["b",128,0],["b",256,0],["b",384,0],["b",512,0],["b",640,0],["b",768,0],["b",896,0],["p",0,0],["p",1,0],["p",2,0],["p",3,0],["x",0,0],["x",1,0],["h",0,0],["p",3,256],["x",2,0],["h",1,0],["y",0,0],["x",3,0],["h",2,0],["y",1,0],["p",3,512],["x",4,0],["h",3,0],["y",2,0],["p",3,768],["x",5,0],["h",4,0],["y",3,0],["h",5,0],["y",4,0],["y",5,0],["g",0,0],["g",0,1],["g",0,2],["g",256,0],["g",256,1],["g",256,2],["g",0,3],["g",512,0],["g",512,1],["g",512,2],["g",512,3],["g",768,0],["g",768,1]]
-TAB_A = 512
-TAGS = {}
-HOLD = {0: 768}
-LAST = [256,256,256,256]
-PRE_STEPS = []
-GATE_W = {(0, 3): 512, (512, 2): 512, (512, 3): 512}
-BANKS = 8
-PROBES = []
+H_LAG, Y_LAG = 1, 3
 
 
 def load_scale_rows(nc, plane, rows):
@@ -59,15 +42,6 @@ def entries(offsets, j0, count):
     return offsets[:, j0 // GROUP : (j0 + count) // GROUP]
 
 
-def starts(widths):
-    return {sum(widths[:n]): w for n, w in enumerate(widths)}
-
-
-def within(parts, j0):
-    p0 = max(p for p in parts if p <= j0)
-    return parts[p0], j0 - p0
-
-
 def tile_list_htabg_max_gateL_kernel(
     tc, tab_words, tab_scales, xT, wgt2, wa_words, wa_scales, wb, wd_words, wd_scales, gT, offs, offs2, out
 ):
@@ -76,19 +50,14 @@ def tile_list_htabg_max_gateL_kernel(
         lists = ctx.enter_context(tc.tile_pool(name="lists", bufs=1))
         keep = ctx.enter_context(tc.tile_pool(name="keep", bufs=1))
         psum = ctx.enter_context(tc.psum_pool(name="psum", bufs=1))
-        used = []
+        banks_taken = []
 
         def tile(name, shape, dtype, tag=None):
-            return keep.tile(shape, dtype, name=name, tag=TAGS.get(name, tag or name), align_bytes=64)
+            return keep.tile(shape, dtype, name=name, tag=tag or name, align_bytes=64)
 
         def next_bank():
-            used.append(len(used))
-            return psum.tile([P, PACK, BANK_J], F32, name=f"bank{len(used) % BANKS}")
-
-        def probe(name, ap):
-            if name in PROBES:
-                clock = tile("clock_" + name, [P, 1], ap.dtype)
-                nc.gpsimd.tensor_copy(out=clock[:], in_=ap)
+            banks_taken.append(None)
+            return psum.tile([P, PACK, BANK_J], F32, name=f"bank{len(banks_taken) % BANKS}")
 
         idx = lists.tile([P, J // GROUP], U16, name="idx")
         idx2 = lists.tile([P, J // GROUP], U16, name="idx2")
@@ -109,35 +78,26 @@ def tile_list_htabg_max_gateL_kernel(
         x_planes = [tile(f"x{i}", [P, T], F32) for i in range(PACK)]
         gates = [tile(f"g{b}", [P, T], F32) for b in range(OUT_BLOCKS)]
 
-        tab_rows = tab_words[0].rearrange("p t i -> p (t i)").bitcast(I32)
-        loads = {
-            "wgt": lambda: nc.sync.dma_start(
-                out=wgt_rows[:],
-                in_=wgt2.rearrange("(e s) j -> e s j", s=WGT_COPIES)[:, 0, :].rearrange("e (u c) -> e u c", c=P),
-            ),
-            "wa": lambda: nc.sync.dma_start(out=wa_w_raw[:], in_=wa_words[0].rearrange("p r i -> p (r i)").bitcast(I32)),
-            "idx": lambda: nc.sync.dma_start(idx[:], offs),
-            "idx2": lambda: nc.sync.dma_start(idx2[:], offs2),
-            "tab_s": lambda: load_scale_rows(nc, tab_s, tab_scales),
-            "wa_s": lambda: load_scale_rows(nc, wa_s_raw, wa_scales),
-            "wd_s": lambda: load_scale_rows(nc, wd_s, wd_scales),
-            "tab": lambda: nc.sync.dma_start(out=tab_w[:], in_=tab_words[0].rearrange("p t i -> p (t i)").bitcast(I32)),
-            "tabA": lambda: nc.sync.dma_start(out=tab_w[:, 0:TAB_A], in_=tab_rows[:, 0:TAB_A]),
-            "tabB": lambda: nc.sync.dma_start(out=tab_w[:, TAB_A:T], in_=tab_rows[:, TAB_A:T]),
-            "wb": lambda: nc.sync.dma_start(out=wb_raw[:], in_=wb.rearrange("(p i) r -> p i r", i=PACK)),
-            "wd": lambda: nc.sync.dma_start(out=wd_w[:].bitcast(I32), in_=wd_words[0].bitcast(I32)),
-        }
-        for name in ORDER:
-            if name[0] == "x":
-                nc.sync.dma_start(out=x_planes[int(name[1])][:], in_=x_rows[:, int(name[1]), :])
-            elif name[0] == "g":
-                b = int(name[1])
-                nc.sync.dma_start(out=gates[b][:], in_=gT[b * P : (b + 1) * P, :])
-            else:
-                loads[name]()
+        nc.sync.dma_start(
+            out=wgt_rows[:],
+            in_=wgt2.rearrange("(e s) j -> e s j", s=WGT_COPIES)[:, 0, :].rearrange("e (u c) -> e u c", c=P),
+        )
+        nc.sync.dma_start(out=wa_w_raw[:], in_=wa_words[0].rearrange("p r i -> p (r i)").bitcast(I32))
+        nc.sync.dma_start(idx[:], offs)
+        load_scale_rows(nc, tab_s, tab_scales)
+        nc.sync.dma_start(out=tab_w[:], in_=tab_words[0].rearrange("p t i -> p (t i)").bitcast(I32))
+        load_scale_rows(nc, wa_s_raw, wa_scales)
+        nc.sync.dma_start(idx2[:], offs2)
+        nc.sync.dma_start(out=x_planes[0][:], in_=x_rows[:, 0, :])
+        nc.sync.dma_start(out=wb_raw[:], in_=wb.rearrange("(p i) r -> p i r", i=PACK))
+        for i in range(1, PACK):
+            if i == PACK // 2:
+                load_scale_rows(nc, wd_s, wd_scales)
+            nc.sync.dma_start(out=x_planes[i][:], in_=x_rows[:, i, :])
+        nc.sync.dma_start(out=wd_w[:].bitcast(I32), in_=wd_words[0].bitcast(I32))
+        for b in range(OUT_BLOCKS):
+            nc.sync.dma_start(out=gates[b][:], in_=gT[b * P : (b + 1) * P, :])
 
-        probe("x3", x_planes[3][:, 0:1])
-        probe("x1", x_planes[1][:, 0:1])
         identity = tile("identity", [P, P], F32)
         make_identity(nc, identity[:])
         turned = next_bank()
@@ -150,38 +110,33 @@ def tile_list_htabg_max_gateL_kernel(
             .unsqueeze(3)
             .to_broadcast([P, WGT_BLOCKS, P // WGT_COPIES, WGT_COPIES]),
         )
-        for u0 in range(0, WGT_BLOCKS, OUT_BLOCKS):
+        for u0 in range(0, WGT_BLOCKS, PACK):
             back = next_bank()
-            for u in range(OUT_BLOCKS):
+            for u in range(PACK):
                 nc.tensor.transpose(back[:, u, :], spread[:, u0 + u, :, :].rearrange("c row a -> c (row a)"), identity[:])
-            nc.scalar.copy(out=wgt[:, u0 * P : (u0 + OUT_BLOCKS) * P], in_=back[:].rearrange("p u c -> p (u c)"))
-        probe("wgt", wgt[:, J - 1 : J])
+            nc.scalar.copy(out=wgt[:, u0 * P : (u0 + PACK) * P], in_=back[:].rearrange("p u c -> p (u c)"))
 
         v_s = tile("v_s", [P, J], U8)
         nc.vector.tensor_copy(v_s[:], tab_s[:].indirect(idx[:]))
-        probe("v_s", v_s[:, J - 4 : J].bitcast(I32))
 
         wb_w = tile("wb_w", [P, R], U32)
         wb_s = tile("wb_s", [P, R], U8)
-        for half in range(2):
-            on_vector = half * 2 >= PACK - WB_VECTOR
-            copy = nc.vector.tensor_copy if on_vector else nc.scalar.copy
-            wb_woven = tile(f"wb_bf{half}", [P, R // 2 * PACK], BF16, tag=None if half else "spread")
+        for half, (copy, tag) in enumerate(((nc.scalar.copy, "spread"), (nc.vector.tensor_copy, None))):
+            wb_woven = tile(f"wb_woven{half}", [P, R // 2 * PACK], BF16, tag)
             copy(
                 out=wb_woven[:].rearrange("p (t m i) -> p m i t", t=2, i=PACK),
                 in_=wb_raw[:].rearrange("p i (m t) -> p m i t", t=PACK)[:, :, :, 2 * half : 2 * half + 2],
             )
             dealt = slice(half * R // 2, (half + 1) * R // 2)
             nc.vector.quantize_mx(out=wb_w[:, dealt].bitcast(FP8X4), scales=wb_s[:, dealt], in_=wb_woven[:])
-        probe("wb_w", wb_w[:, R - 1 : R])
 
-        def product(w_words, w_scales, words, scales):
+        def product(stationary, stationary_scales, words, scales):
             bank = next_bank()
-            for t in range(PACK):
+            for u in range(PACK):
                 nc.tensor.matmul_mx(
-                    out=bank[:, t, :],
-                    lhsT=w_words(t),
-                    lhsT_scale=w_scales[:, t * P : (t + 1) * P],
+                    out=bank[:, u, :],
+                    lhsT=stationary(u),
+                    lhsT_scale=stationary_scales[:, u * P : (u + 1) * P],
                     rhs=words.bitcast(FP8X4),
                     rhs_scale=scales,
                     start=True,
@@ -197,121 +152,102 @@ def tile_list_htabg_max_gateL_kernel(
             width = woven.shape[1]
             words = tile(name + "_w", [P, width], U32)
             scales = tile(name + "_s", [P, width], U8)
-            nc.vector.quantize_mx(
-                out=words[:].bitcast(FP8X4), scales=scales[:], in_=woven[:].rearrange("p j t -> p (j t)")
-            )
+            nc.vector.quantize_mx(out=words[:].bitcast(FP8X4), scales=scales[:], in_=woven.rearrange("p j t -> p (j t)"))
             return words, scales
 
-        y = {j0: tile(f"y{j0}", [P, OUT_BLOCKS, count], F32) for j0, count in starts(GATE_J).items()}
-        yb = {j0: tile(f"yb{j0}", [P, width, PACK], BF16) for j0, width in starts(STEPS).items()}
-        v_pieces = {}
-
-        def look_up(j0, count):
-            v_pieces[j0] = tile(f"v_w{j0}", [P, count], U32)
-            nc.vector.tensor_copy(v_pieces[j0][:], tab_w[:].bitcast(U32).indirect(entries(idx, j0, count)))
-
-        def make_yb(j0):
-            into, at = within(yb, j0)
-            words, w0 = within(v_pieces, j0)
-            sums = first_layer(wb_w, wb_s, words[:, w0 : w0 + BANK_J], v_s[:, j0 : j0 + BANK_J])
-            nc.scalar.copy(out=into[:, at : at + BANK_J, :], in_=sums)
-
-        pieces = starts(PIECES)
-        xg = {j0: tile(f"picked{j0}", [P, PACK * count], F32)[:].rearrange("p (i j) -> p i j", i=PACK) for j0, count in pieces.items()}
-
-        def pick(i, j0, count):
-            nc.vector.tensor_tensor(
-                within(xg, j0)[0][:, i, within(xg, j0)[1] : within(xg, j0)[1] + count], x_planes[i][:].indirect(entries(idx2, j0, count)), wgt[:, j0 : j0 + count], MULT
-            )
-
-        steps = list(starts(STEPS).items())
-        x_woven = {}
-
-        def woven_tile(step):
-            width = STEPS[step]
-            if step not in x_woven:
-                if step in HOLD:
-                    held, at = within(xg, HOLD[step])
-                    room = held[:, PACK - 1, at : at + 2 * width].bitcast(BF16)
-                else:
-                    room = tile(f"xb{step}", [P, width * PACK], BF16)[:]
-                x_woven[step] = room.rearrange("p (j i) -> p j i", i=PACK)
-            return x_woven[step]
-
-        def weave(step, i0, i1):
-            j0, width = steps[step]
-            source, at = within(xg, j0)
-            nc.scalar.copy(
-                out=woven_tile(step)[:, :, i0:i1].rearrange("p (u v) i -> p u i v", v=4),
-                in_=source[:, i0:i1, at : at + width].rearrange("p i (u v) -> p u i v", v=4),
-            )
+        steps = [(sum(STEPS[:step]), width) for step, width in enumerate(STEPS)]
+        y = [tile(f"y{half}", [P, OUT_BLOCKS, HALF], F32) for half in range(2)]
+        yb = [tile(f"yb{step}", [P, width, PACK], BF16) for step, width in enumerate(STEPS)]
+        xg = tile("xg", [P, PACK * J], F32)[:].rearrange("p (i j) -> p i j", i=PACK)
 
         wa_w = tile("wa_w", [P, R], I32)
         wa_s = tile("wa_s", [P, R], U8)
+        for engine, ordered, raw in ((nc.vector, wa_w, wa_w_raw), (nc.gpsimd, wa_s, wa_s_raw)):
+            engine.tensor_copy(
+                out=ordered[:].rearrange("p (t m) -> p t m", t=PACK), in_=raw[:].rearrange("p (m t) -> p t m", t=PACK)
+            )
 
-        def deal(which):
-            into, raw = ((wa_w, wa_w_raw), (wa_s, wa_s_raw))[which]
-            (nc.vector, nc.gpsimd)[which].tensor_copy(out=into[:].rearrange("p (t m) -> p t m", t=PACK), in_=raw[:].rearrange("p (m t) -> p t m", t=PACK))
+        v_w = tile("v_w", [P, J], U32)
+        nc.vector.tensor_copy(v_w[:], tab_w[:].bitcast(U32).indirect(idx[:]))
+        for step, (j0, width) in enumerate(steps):
+            for u in range(0, width, BANK_J):
+                cols = slice(j0 + u, j0 + u + BANK_J)
+                sums = first_layer(wb_w, wb_s, v_w[:, cols], v_s[:, cols])
+                nc.scalar.copy(out=yb[step][:, u : u + BANK_J, :], in_=sums)
 
-        x_q = {}
-        h_q = {}
+        def pick(i, j0, count):
+            cols = slice(j0, j0 + count)
+            nc.vector.tensor_tensor(xg[:, i, cols], x_planes[i][:].indirect(entries(idx2, j0, count)), wgt[:, cols], MULT)
 
-        def stage_x(step):
+        for i in range(PACK - 1):
+            pick(i, 0, J)
+
+        def make_xg(step):
             j0, width = steps[step]
-            weave(step, 2 if step in PRE_STEPS else 0, PACK)
-            x_q[step] = quantise(f"xq{step}", x_woven[step])
-            probe(f"xq{step}", x_q[step][0][:, 0:1])
+            if j0 % QUARTER == 0:
+                pick(PACK - 1, j0, QUARTER)
+            if step == 0:
+                woven = xg[:, PACK - 1, J - QUARTER : J].bitcast(BF16)
+            else:
+                woven = tile(f"x_woven{step}", [P, width * PACK], BF16)[:]
+            woven = woven.rearrange("p (j i) -> p j i", i=PACK)
+            nc.scalar.copy(
+                out=woven.rearrange("p (u v) i -> p u i v", v=4),
+                in_=xg[:, :, j0 : j0 + width].rearrange("p i (u v) -> p u i v", v=4),
+            )
+            return quantise(f"xq{step}", woven)
 
-        def stage_h(step):
-            j0, width = steps[step]
-            x_w, x_s = x_q[step]
+        def make_h(step, x_w, x_s):
+            width = STEPS[step]
             banks = [slice(u, u + BANK_J) for u in range(0, width, BANK_J)]
             h = tile(f"h{step}", [P, width, PACK], BF16)
             if step < PSUM_MAX_STEPS:
                 for cols in banks:
                     ya_sums = first_layer(wa_w, wa_s, x_w[:, cols], x_s[:, cols])
-                    nc.vector.tensor_tensor(h[:, cols, :], ya_sums, yb[j0][:, cols, :], MAX)
+                    nc.vector.tensor_tensor(h[:, cols, :], ya_sums, yb[step][:, cols, :], MAX)
             else:
                 ya = tile(f"ya{step}", [P, width, PACK], BF16)
                 for cols in banks:
                     nc.scalar.copy(out=ya[:, cols, :], in_=first_layer(wa_w, wa_s, x_w[:, cols], x_s[:, cols]))
-                nc.vector.tensor_tensor(h[:], ya[:], yb[j0][:], MAX)
-            h_q[step] = quantise(f"hq{step}", h)
+                nc.vector.tensor_tensor(h[:], ya[:], yb[step][:], MAX)
+            return quantise(f"hq{step}", h[:])
 
-        def stage_y(step):
+        def make_y(step, h_w, h_s):
             j0, width = steps[step]
-            h_w, h_s = h_q[step]
             for u in range(0, width, BANK_J):
                 cols = slice(u, u + BANK_J)
-                bank = product(lambda b: wd_w[:, 2 * b * P : 2 * (b + 1) * P].bitcast(FP4X4), wd_s, h_w[:, cols], h_s[:, cols])
-                into, at = within(y, j0 + u)
-                nc.scalar.copy(out=into[:, :, at : at + BANK_J], in_=bank[:])
-            probe(f"y{step}", into[:, 0, at : at + 1])
+                bank = product(
+                    lambda b: wd_w[:, 2 * b * P : 2 * (b + 1) * P].bitcast(FP4X4), wd_s, h_w[:, cols], h_s[:, cols]
+                )
+                at = (j0 + u) % HALF
+                nc.scalar.copy(out=y[j0 // HALF][:, :, at : at + BANK_J], in_=bank[:])
 
-        def gate(j0, b):
-            count = GATE_W.get((j0, b), 256)
-            sums, at = within(y, j0)
-            gated = tile(f"o{j0}_{b}", [P, count], F32)
-            nc.vector.tensor_tensor(gated[:], gates[b][:].indirect(entries(idx, j0, count)), sums[:, b, at : at + count], MULT)
+        x_quantised = []
+        h_quantised = []
+        for turn in range(len(STEPS) + Y_LAG):
+            if turn < len(STEPS):
+                x_quantised.append(make_xg(turn))
+            if 0 <= turn - H_LAG < len(STEPS):
+                h_quantised.append(make_h(turn - H_LAG, *x_quantised[turn - H_LAG]))
+            if 0 <= turn - Y_LAG:
+                make_y(turn - Y_LAG, *h_quantised[turn - Y_LAG])
+
+        def gate(b, j0, count):
+            gated = tile(f"gated{b}_{j0}", [P, count], F32)
+            at = j0 % HALF
+            sums = y[j0 // HALF][:, b, at : at + count]
+            nc.vector.tensor_tensor(gated[:], gates[b][:].indirect(entries(idx, j0, count)), sums, MULT)
             nc.sync.dma_start(out=out[b * P : (b + 1) * P, j0 : j0 + count], in_=gated[:])
 
-        for what, a, b in PLAN:
-            if what == "p":
-                pick(a, b, pieces[b] if a < PACK - 1 else starts(LAST)[b])
-                probe(f"p{a}_{b}", within(xg, b)[0][:, a, within(xg, b)[1] : within(xg, b)[1] + 1])
-            elif what == "w":
-                look_up(a, starts(WORDS)[a])
-            elif what == "d":
-                deal(a)
-            elif what == "x":
-                stage_x(a)
-            elif what == "h":
-                stage_h(a)
-            elif what == "y":
-                stage_y(a)
-            elif what == "b":
-                make_yb(a)
-            elif what == "e":
-                weave(a, 0, 2)
-            else:
-                gate(a, b)
+        last = OUT_BLOCKS - 1
+        for j0 in (0, QUARTER):
+            for b in range(last):
+                gate(b, j0, QUARTER)
+        gate(last, 0, HALF)
+        early, late = range(OUT_BLOCKS // 2), range(OUT_BLOCKS // 2, OUT_BLOCKS)
+        for b in early:
+            gate(b, HALF, QUARTER)
+        for b in late:
+            gate(b, HALF, HALF)
+        for b in early:
+            gate(b, HALF + QUARTER, QUARTER)

@@ -29,7 +29,10 @@ WGT_COPIES = 8
 HALF, QUARTER = J // 2, J // 4
 
 STEPS = (BANK_J,) * 4 + (2 * BANK_J,) * 2
-PSUM_MAX_STEPS = 4
+PSUM_MAX_STEPS = 3
+EARLY_STEPS = 4
+BORROWED = {"x_woven0": 3}
+SHARED = {"xg": "wb_woven1"}
 H_LAG, Y_LAG = 1, 3
 
 
@@ -53,7 +56,7 @@ def tile_list_htabg_max_gateL_kernel(
         banks_taken = []
 
         def tile(name, shape, dtype, tag=None):
-            return keep.tile(shape, dtype, name=name, tag=tag or name, align_bytes=64)
+            return keep.tile(shape, dtype, name=name, tag=tag or SHARED.get(name, name), align_bytes=64)
 
         def next_bank():
             banks_taken.append(None)
@@ -88,12 +91,12 @@ def tile_list_htabg_max_gateL_kernel(
         nc.sync.dma_start(out=tab_w[:], in_=tab_words[0].rearrange("p t i -> p (t i)").bitcast(I32))
         load_scale_rows(nc, wa_s_raw, wa_scales)
         nc.sync.dma_start(idx2[:], offs2)
-        nc.sync.dma_start(out=x_planes[0][:], in_=x_rows[:, 0, :])
         nc.sync.dma_start(out=wb_raw[:], in_=wb.rearrange("(p i) r -> p i r", i=PACK))
-        for i in range(1, PACK):
-            if i == PACK // 2:
-                load_scale_rows(nc, wd_s, wd_scales)
-            nc.sync.dma_start(out=x_planes[i][:], in_=x_rows[:, i, :])
+        nc.sync.dma_start(out=x_planes[0][:], in_=x_rows[:, 0, :])
+        nc.sync.dma_start(out=x_planes[1][:], in_=x_rows[:, 1, :])
+        load_scale_rows(nc, wd_s, wd_scales)
+        nc.sync.dma_start(out=x_planes[2][:], in_=x_rows[:, 2, :])
+        nc.sync.dma_start(out=x_planes[3][:], in_=x_rows[:, 3, :])
         nc.sync.dma_start(out=wd_w[:].bitcast(I32), in_=wd_words[0].bitcast(I32))
         for b in range(OUT_BLOCKS):
             nc.sync.dma_start(out=gates[b][:], in_=gT[b * P : (b + 1) * P, :])
@@ -162,10 +165,13 @@ def tile_list_htabg_max_gateL_kernel(
 
         wa_w = tile("wa_w", [P, R], I32)
         wa_s = tile("wa_s", [P, R], U8)
-        for engine, ordered, raw in ((nc.vector, wa_w, wa_w_raw), (nc.gpsimd, wa_s, wa_s_raw)):
+        def deal(engine, ordered, raw):
             engine.tensor_copy(
                 out=ordered[:].rearrange("p (t m) -> p t m", t=PACK), in_=raw[:].rearrange("p (m t) -> p t m", t=PACK)
             )
+
+        deal(nc.gpsimd, wa_s, wa_s_raw)
+        deal(nc.vector, wa_w, wa_w_raw)
 
         v_w = tile("v_w", [P, J], U32)
         nc.vector.tensor_copy(v_w[:], tab_w[:].bitcast(U32).indirect(idx[:]))
@@ -179,28 +185,42 @@ def tile_list_htabg_max_gateL_kernel(
             cols = slice(j0, j0 + count)
             nc.vector.tensor_tensor(xg[:, i, cols], x_planes[i][:].indirect(entries(idx2, j0, count)), wgt[:, cols], MULT)
 
+        def bf16_tile(name, width):
+            if name in BORROWED:
+                plane, quarter = divmod(BORROWED[name], PACK)
+                return xg[:, PACK - 1 - plane, quarter * QUARTER : (quarter + 1) * QUARTER].bitcast(BF16)
+            return tile(name, [P, width * PACK], BF16)[:]
+
+        x_woven = {step: bf16_tile(f"x_woven{step}", STEPS[step]) for step in range(EARLY_STEPS)}
+
+        def weave(step, first, count):
+            j0, width = steps[step]
+            planes = slice(first, first + count)
+            nc.scalar.copy(
+                out=x_woven[step].rearrange("p (u v i) -> p u i v", v=4, i=PACK)[:, :, planes, :],
+                in_=xg[:, planes, j0 : j0 + width].rearrange("p i (u v) -> p u i v", v=4),
+            )
+
         for i in range(PACK - 1):
             pick(i, 0, J)
+            if i == 1:
+                for step in range(EARLY_STEPS):
+                    weave(step, 0, 2)
 
         def make_xg(step):
             j0, width = steps[step]
-            if j0 % QUARTER == 0:
-                pick(PACK - 1, j0, QUARTER)
-            if step == 0:
-                woven = xg[:, PACK - 1, J - QUARTER : J].bitcast(BF16)
+            if step < EARLY_STEPS:
+                weave(step, 2, 2)
             else:
-                woven = tile(f"x_woven{step}", [P, width * PACK], BF16)[:]
-            woven = woven.rearrange("p (j i) -> p j i", i=PACK)
-            nc.scalar.copy(
-                out=woven.rearrange("p (u v) i -> p u i v", v=4),
-                in_=xg[:, :, j0 : j0 + width].rearrange("p i (u v) -> p u i v", v=4),
-            )
+                x_woven[step] = bf16_tile(f"x_woven{step}", width)
+                weave(step, 0, PACK)
+            woven = x_woven[step].rearrange("p (j i) -> p j i", i=PACK)
             return quantise(f"xq{step}", woven)
 
         def make_h(step, x_w, x_s):
             width = STEPS[step]
             banks = [slice(u, u + BANK_J) for u in range(0, width, BANK_J)]
-            h = tile(f"h{step}", [P, width, PACK], BF16)
+            h = bf16_tile(f"h{step}", width).rearrange("p (j t) -> p j t", t=PACK)
             if step < PSUM_MAX_STEPS:
                 for cols in banks:
                     ya_sums = first_layer(wa_w, wa_s, x_w[:, cols], x_s[:, cols])
@@ -209,8 +229,8 @@ def tile_list_htabg_max_gateL_kernel(
                 ya = tile(f"ya{step}", [P, width, PACK], BF16)
                 for cols in banks:
                     nc.scalar.copy(out=ya[:, cols, :], in_=first_layer(wa_w, wa_s, x_w[:, cols], x_s[:, cols]))
-                nc.vector.tensor_tensor(h[:], ya[:], yb[step][:], MAX)
-            return quantise(f"hq{step}", h[:])
+                nc.vector.tensor_tensor(h, ya[:], yb[step][:], MAX)
+            return h
 
         def make_y(step, h_w, h_s):
             j0, width = steps[step]
@@ -222,32 +242,66 @@ def tile_list_htabg_max_gateL_kernel(
                 at = (j0 + u) % HALF
                 nc.scalar.copy(out=y[j0 // HALF][:, :, at : at + BANK_J], in_=bank[:])
 
-        x_quantised = []
-        h_quantised = []
-        for turn in range(len(STEPS) + Y_LAG):
-            if turn < len(STEPS):
-                x_quantised.append(make_xg(turn))
-            if 0 <= turn - H_LAG < len(STEPS):
-                h_quantised.append(make_h(turn - H_LAG, *x_quantised[turn - H_LAG]))
-            if 0 <= turn - Y_LAG:
-                make_y(turn - Y_LAG, *h_quantised[turn - Y_LAG])
+        gated_tiles = {}
 
         def gate(b, j0, count):
-            gated = tile(f"gated{b}_{j0}", [P, count], F32)
+            width = max(count, QUARTER)
+            first = j0 - j0 % QUARTER
+            if j0 == first:
+                gated_tiles[b] = tile(f"gated{b}_{j0}", [P, width], F32)
+            gated = gated_tiles[b][:, j0 - first : j0 - first + count]
             at = j0 % HALF
             sums = y[j0 // HALF][:, b, at : at + count]
-            nc.vector.tensor_tensor(gated[:], gates[b][:].indirect(entries(idx, j0, count)), sums, MULT)
-            nc.sync.dma_start(out=out[b * P : (b + 1) * P, j0 : j0 + count], in_=gated[:])
+            nc.vector.tensor_tensor(gated, gates[b][:].indirect(entries(idx, j0, count)), sums, MULT)
+            if j0 + count == first + width:
+                nc.sync.dma_start(out=out[b * P : (b + 1) * P, first : first + width], in_=gated_tiles[b][:])
 
-        last = OUT_BLOCKS - 1
-        for j0 in (0, QUARTER):
-            for b in range(last):
-                gate(b, j0, QUARTER)
-        gate(last, 0, HALF)
-        early, late = range(OUT_BLOCKS // 2), range(OUT_BLOCKS // 2, OUT_BLOCKS)
-        for b in early:
-            gate(b, HALF, QUARTER)
-        for b in late:
-            gate(b, HALF, HALF)
-        for b in early:
-            gate(b, HALF + QUARTER, QUARTER)
+        x_quantised = {}
+        h_values = {}
+        h_quantised = {}
+        pick(PACK - 1, 0, 256)
+        x_quantised[0] = make_xg(0)
+        x_quantised[1] = make_xg(1)
+        h_values[0] = make_h(0, *x_quantised[0])
+        h_quantised[0] = quantise("hq0", h_values[0])
+        pick(PACK - 1, 256, 256)
+        x_quantised[2] = make_xg(2)
+        h_values[1] = make_h(1, *x_quantised[1])
+        h_quantised[1] = quantise("hq1", h_values[1])
+        x_quantised[3] = make_xg(3)
+        h_values[2] = make_h(2, *x_quantised[2])
+        h_quantised[2] = quantise("hq2", h_values[2])
+        make_y(0, *h_quantised[0])
+        pick(PACK - 1, 512, 256)
+        x_quantised[4] = make_xg(4)
+        h_values[3] = make_h(3, *x_quantised[3])
+        h_quantised[3] = quantise("hq3", h_values[3])
+        make_y(1, *h_quantised[1])
+        pick(PACK - 1, 768, 256)
+        x_quantised[5] = make_xg(5)
+        h_values[4] = make_h(4, *x_quantised[4])
+        h_quantised[4] = quantise("hq4", h_values[4])
+        make_y(2, *h_quantised[2])
+        h_values[5] = make_h(5, *x_quantised[5])
+        h_quantised[5] = quantise("hq5", h_values[5])
+        make_y(3, *h_quantised[3])
+        make_y(4, *h_quantised[4])
+        make_y(5, *h_quantised[5])
+        gate(0, 0, 128)
+        gate(1, 0, 128)
+        gate(0, 128, 128)
+        gate(1, 128, 128)
+        gate(2, 0, 256)
+        gate(0, 256, 128)
+        gate(1, 256, 128)
+        gate(2, 256, 128)
+        gate(0, 384, 128)
+        gate(1, 384, 128)
+        gate(2, 384, 128)
+        gate(3, 0, 512)
+        gate(0, 512, 256)
+        gate(1, 512, 256)
+        gate(2, 512, 512)
+        gate(3, 512, 512)
+        gate(0, 768, 256)
+        gate(1, 768, 256)

@@ -28,17 +28,17 @@ WGT_BLOCKS = J // P
 WGT_COPIES = 8
 HALF, QUARTER = J // 2, J // 4
 
-STEPS = (BANK_J,) * 4 + (2 * BANK_J,) * 2
-PSUM_MAX_STEPS = 3
-EARLY_STEPS = 4
+STEPS = (128,) * 4 + (256,) * 2
+PSUM_MAX_STEPS = 2
+EARLY_STEPS = 5
 BORROWED = {"x_woven0": 3}
+TAB_FIRST = 512
 SHARED = {"xg": "wb_woven1"}
-H_LAG, Y_LAG = 1, 3
 
 
-def load_scale_rows(nc, plane, rows):
+def load_scale_rows(queue, plane, rows):
     for q in range(QUADRANTS):
-        nc.sync.dma_start(out=plane[32 * q : 32 * q + 4, :].bitcast(I32), in_=rows[0, 4 * q : 4 * q + 4, :].bitcast(I32))
+        queue.dma_start(out=plane[32 * q : 32 * q + 4, :].bitcast(I32), in_=rows[0, 4 * q : 4 * q + 4, :].bitcast(I32))
 
 
 def entries(offsets, j0, count):
@@ -81,28 +81,31 @@ def tile_list_htabg_max_gateL_kernel(
         x_planes = [tile(f"x{i}", [P, T], F32) for i in range(PACK)]
         gates = [tile(f"g{b}", [P, T], F32) for b in range(OUT_BLOCKS)]
 
+        tab_rows = tab_words[0].rearrange("p t i -> p (t i)").bitcast(I32)
+        identity = tile("identity", [P, P], F32)
+        make_identity(nc, identity[:])
         nc.sync.dma_start(
             out=wgt_rows[:],
             in_=wgt2.rearrange("(e s) j -> e s j", s=WGT_COPIES)[:, 0, :].rearrange("e (u c) -> e u c", c=P),
         )
         nc.sync.dma_start(out=wa_w_raw[:], in_=wa_words[0].rearrange("p r i -> p (r i)").bitcast(I32))
         nc.sync.dma_start(idx[:], offs)
-        load_scale_rows(nc, tab_s, tab_scales)
-        nc.sync.dma_start(out=tab_w[:], in_=tab_words[0].rearrange("p t i -> p (t i)").bitcast(I32))
-        load_scale_rows(nc, wa_s_raw, wa_scales)
+        load_scale_rows(nc.sync, tab_s, tab_scales)
+        nc.sync.dma_start(out=tab_w[:], in_=tab_rows)
+        load_scale_rows(nc.sync, wa_s_raw, wa_scales)
         nc.sync.dma_start(idx2[:], offs2)
         nc.sync.dma_start(out=wb_raw[:], in_=wb.rearrange("(p i) r -> p i r", i=PACK))
         nc.sync.dma_start(out=x_planes[0][:], in_=x_rows[:, 0, :])
         nc.sync.dma_start(out=x_planes[1][:], in_=x_rows[:, 1, :])
-        load_scale_rows(nc, wd_s, wd_scales)
+        load_scale_rows(nc.sync, wd_s, wd_scales)
         nc.sync.dma_start(out=x_planes[2][:], in_=x_rows[:, 2, :])
         nc.sync.dma_start(out=x_planes[3][:], in_=x_rows[:, 3, :])
         nc.sync.dma_start(out=wd_w[:].bitcast(I32), in_=wd_words[0].bitcast(I32))
-        for b in range(OUT_BLOCKS):
-            nc.sync.dma_start(out=gates[b][:], in_=gT[b * P : (b + 1) * P, :])
+        nc.sync.dma_start(out=gates[0][:], in_=gT[0 * P : 1 * P, :])
+        nc.sync.dma_start(out=gates[1][:], in_=gT[1 * P : 2 * P, :])
+        nc.sync.dma_start(out=gates[2][:], in_=gT[2 * P : 3 * P, :])
+        nc.sync.dma_start(out=gates[3][:], in_=gT[3 * P : 4 * P, :])
 
-        identity = tile("identity", [P, P], F32)
-        make_identity(nc, identity[:])
         turned = next_bank()
         nc.tensor.transpose(turned[:, 0, :], wgt_rows[:], identity[:])
         spread = tile("spread", [P, WGT_BLOCKS, P // WGT_COPIES, WGT_COPIES], F32)
@@ -165,16 +168,14 @@ def tile_list_htabg_max_gateL_kernel(
 
         wa_w = tile("wa_w", [P, R], I32)
         wa_s = tile("wa_s", [P, R], U8)
-        def deal(engine, ordered, raw):
-            engine.tensor_copy(
-                out=ordered[:].rearrange("p (t m) -> p t m", t=PACK), in_=raw[:].rearrange("p (m t) -> p t m", t=PACK)
-            )
+        def deal(copy, ordered, raw):
+            copy(out=ordered.rearrange("p (t m) -> p t m", t=PACK), in_=raw.rearrange("p (m t) -> p t m", t=PACK))
 
-        deal(nc.gpsimd, wa_s, wa_s_raw)
-        deal(nc.vector, wa_w, wa_w_raw)
+        deal(nc.gpsimd.tensor_copy, wa_s[:], wa_s_raw[:])
+        deal(nc.vector.tensor_copy, wa_w[:].bitcast(U32), wa_w_raw[:].bitcast(U32))
 
         v_w = tile("v_w", [P, J], U32)
-        nc.vector.tensor_copy(v_w[:], tab_w[:].bitcast(U32).indirect(idx[:]))
+        nc.vector.tensor_copy(v_w[:, 0:1024], tab_w[:].bitcast(U32).indirect(entries(idx, 0, 1024)))
         for step, (j0, width) in enumerate(steps):
             for u in range(0, width, BANK_J):
                 cols = slice(j0 + u, j0 + u + BANK_J)
@@ -245,8 +246,8 @@ def tile_list_htabg_max_gateL_kernel(
         gated_tiles = {}
 
         def gate(b, j0, count):
-            width = max(count, QUARTER)
-            first = j0 - j0 % QUARTER
+            width = max(count, QUARTER) if j0 < HALF else count
+            first = j0 - j0 % QUARTER if j0 < HALF else j0
             if j0 == first:
                 gated_tiles[b] = tile(f"gated{b}_{j0}", [P, width], F32)
             gated = gated_tiles[b][:, j0 - first : j0 - first + count]
@@ -256,37 +257,37 @@ def tile_list_htabg_max_gateL_kernel(
             if j0 + count == first + width:
                 nc.sync.dma_start(out=out[b * P : (b + 1) * P, first : first + width], in_=gated_tiles[b][:])
 
-        x_quantised = {}
-        h_values = {}
-        h_quantised = {}
-        pick(PACK - 1, 0, 256)
-        x_quantised[0] = make_xg(0)
-        x_quantised[1] = make_xg(1)
-        h_values[0] = make_h(0, *x_quantised[0])
-        h_quantised[0] = quantise("hq0", h_values[0])
-        pick(PACK - 1, 256, 256)
-        x_quantised[2] = make_xg(2)
-        h_values[1] = make_h(1, *x_quantised[1])
-        h_quantised[1] = quantise("hq1", h_values[1])
-        x_quantised[3] = make_xg(3)
-        h_values[2] = make_h(2, *x_quantised[2])
-        h_quantised[2] = quantise("hq2", h_values[2])
-        make_y(0, *h_quantised[0])
-        pick(PACK - 1, 512, 256)
-        x_quantised[4] = make_xg(4)
-        h_values[3] = make_h(3, *x_quantised[3])
-        h_quantised[3] = quantise("hq3", h_values[3])
-        make_y(1, *h_quantised[1])
-        pick(PACK - 1, 768, 256)
-        x_quantised[5] = make_xg(5)
-        h_values[4] = make_h(4, *x_quantised[4])
-        h_quantised[4] = quantise("hq4", h_values[4])
-        make_y(2, *h_quantised[2])
-        h_values[5] = make_h(5, *x_quantised[5])
-        h_quantised[5] = quantise("hq5", h_values[5])
-        make_y(3, *h_quantised[3])
-        make_y(4, *h_quantised[4])
-        make_y(5, *h_quantised[5])
+        xq = {}
+        hv = {}
+        hq = {}
+        pick(3, 0, 256)
+        xq[0] = make_xg(0)
+        xq[1] = make_xg(1)
+        hv[0] = make_h(0, *xq[0])
+        hq[0] = quantise("hq0", hv[0])
+        pick(3, 256, 256)
+        xq[2] = make_xg(2)
+        hv[1] = make_h(1, *xq[1])
+        hq[1] = quantise("hq1", hv[1])
+        xq[3] = make_xg(3)
+        hv[2] = make_h(2, *xq[2])
+        hq[2] = quantise("hq2", hv[2])
+        make_y(0, *hq[0])
+        pick(3, 512, 256)
+        xq[4] = make_xg(4)
+        hv[3] = make_h(3, *xq[3])
+        hq[3] = quantise("hq3", hv[3])
+        make_y(1, *hq[1])
+        pick(3, 768, 256)
+        xq[5] = make_xg(5)
+        hv[4] = make_h(4, *xq[4])
+        hq[4] = quantise("hq4", hv[4])
+        make_y(2, *hq[2])
+        hv[5] = make_h(5, *xq[5])
+        hq[5] = quantise("hq5", hv[5])
+        make_y(3, *hq[3])
+        make_y(4, *hq[4])
+        make_y(5, *hq[5])
         gate(0, 0, 128)
         gate(1, 0, 128)
         gate(0, 128, 128)
@@ -294,14 +295,13 @@ def tile_list_htabg_max_gateL_kernel(
         gate(2, 0, 256)
         gate(0, 256, 128)
         gate(1, 256, 128)
-        gate(2, 256, 128)
         gate(0, 384, 128)
         gate(1, 384, 128)
-        gate(2, 384, 128)
+        gate(2, 256, 256)
         gate(3, 0, 512)
         gate(0, 512, 256)
-        gate(1, 512, 256)
         gate(2, 512, 512)
+        gate(1, 512, 384)
         gate(3, 512, 512)
         gate(0, 768, 256)
-        gate(1, 768, 256)
+        gate(1, 896, 128)

@@ -29,7 +29,7 @@ WGT_COPIES = 8
 HALF, QUARTER = J // 2, J // 4
 
 STEPS = (128,) * 4 + (256,) * 2
-PSUM_MAX_STEPS = 2
+PSUM_MAX_STEPS = 3
 EARLY_STEPS = 5
 BORROWED = {"x_woven0": 3}
 TAB_FIRST = 512
@@ -171,7 +171,7 @@ def tile_list_htabg_max_gateL_kernel(
         def deal(copy, ordered, raw):
             copy(out=ordered.rearrange("p (t m) -> p t m", t=PACK), in_=raw.rearrange("p (m t) -> p t m", t=PACK))
 
-        deal(nc.gpsimd.tensor_copy, wa_s[:], wa_s_raw[:])
+        deal(nc.vector.tensor_copy, wa_s[:], wa_s_raw[:])
         deal(nc.vector.tensor_copy, wa_w[:].bitcast(U32), wa_w_raw[:].bitcast(U32))
 
         v_w = tile("v_w", [P, J], U32)
@@ -249,13 +249,13 @@ def tile_list_htabg_max_gateL_kernel(
             width = max(count, QUARTER) if j0 < HALF else count
             first = j0 - j0 % QUARTER if j0 < HALF else j0
             if j0 == first:
-                gated_tiles[b] = tile(f"gated{b}_{j0}", [P, width], F32)
-            gated = gated_tiles[b][:, j0 - first : j0 - first + count]
+                gated_tiles[b, first] = tile(f"gated{b}_{j0}", [P, width], F32)
+            gated = gated_tiles[b, first][:, j0 - first : j0 - first + count]
             at = j0 % HALF
             sums = y[j0 // HALF][:, b, at : at + count]
             nc.vector.tensor_tensor(gated, gates[b][:].indirect(entries(idx, j0, count)), sums, MULT)
             if j0 + count == first + width:
-                nc.sync.dma_start(out=out[b * P : (b + 1) * P, first : first + width], in_=gated_tiles[b][:])
+                nc.sync.dma_start(out=out[b * P : (b + 1) * P, first : first + width], in_=gated_tiles[b, first][:])
 
         xq = {}
         hv = {}
@@ -263,23 +263,23 @@ def tile_list_htabg_max_gateL_kernel(
         pick(3, 0, 256)
         xq[0] = make_xg(0)
         xq[1] = make_xg(1)
-        hv[0] = make_h(0, *xq[0])
-        hq[0] = quantise("hq0", hv[0])
         pick(3, 256, 256)
         xq[2] = make_xg(2)
+        xq[3] = make_xg(3)
+        hv[0] = make_h(0, *xq[0])
+        hq[0] = quantise("hq0", hv[0])
         hv[1] = make_h(1, *xq[1])
         hq[1] = quantise("hq1", hv[1])
-        xq[3] = make_xg(3)
+        pick(3, 512, 256)
+        xq[4] = make_xg(4)
         hv[2] = make_h(2, *xq[2])
         hq[2] = quantise("hq2", hv[2])
         make_y(0, *hq[0])
-        pick(3, 512, 256)
-        xq[4] = make_xg(4)
+        pick(3, 768, 256)
+        xq[5] = make_xg(5)
         hv[3] = make_h(3, *xq[3])
         hq[3] = quantise("hq3", hv[3])
         make_y(1, *hq[1])
-        pick(3, 768, 256)
-        xq[5] = make_xg(5)
         hv[4] = make_h(4, *xq[4])
         hq[4] = quantise("hq4", hv[4])
         make_y(2, *hq[2])
@@ -289,19 +289,17 @@ def tile_list_htabg_max_gateL_kernel(
         make_y(4, *hq[4])
         make_y(5, *hq[5])
         gate(0, 0, 128)
-        gate(1, 0, 128)
         gate(0, 128, 128)
-        gate(1, 128, 128)
-        gate(2, 0, 256)
+        gate(1, 0, 256)
         gate(0, 256, 128)
         gate(1, 256, 128)
         gate(0, 384, 128)
         gate(1, 384, 128)
-        gate(2, 256, 256)
-        gate(3, 0, 512)
+        gate(2, 0, 512)
         gate(0, 512, 256)
-        gate(2, 512, 512)
         gate(1, 512, 384)
+        gate(3, 0, 512)
+        gate(2, 512, 512)
         gate(3, 512, 512)
         gate(0, 768, 256)
         gate(1, 896, 128)

@@ -171,7 +171,7 @@ def tile_list_htabg_max_gateL_kernel(
         def deal(copy, ordered, raw):
             copy(out=ordered.rearrange("p (t m) -> p t m", t=PACK), in_=raw.rearrange("p (m t) -> p t m", t=PACK))
 
-        deal(nc.vector.tensor_copy, wa_s[:], wa_s_raw[:])
+        deal(nc.gpsimd.tensor_copy, wa_s[:], wa_s_raw[:])
         deal(nc.vector.tensor_copy, wa_w[:].bitcast(U32), wa_w_raw[:].bitcast(U32))
 
         v_w = tile("v_w", [P, J], U32)

@@ -56,7 +56,7 @@ def tile_list_htabg_max_gateL_kernel(
         banks_taken = []
 
         def tile(name, shape, dtype, tag=None):
-            return keep.tile(shape, dtype, name=name, tag=tag or SHARED.get(name, name), align_bytes=64)
+            return keep.tile(shape, dtype, name=name, tag=tag or SHARED.get(name, name), align_bytes=256)
 
         def next_bank():
             banks_taken.append(None)

@@ -28,12 +28,13 @@ WGT_BLOCKS = J // P
 WGT_COPIES = 8
 HALF, QUARTER = J // 2, J // 4
 
-STEPS = (128,) * 4 + (256,) * 2
+STEPS = (BANK_J,) * 4 + (QUARTER,) * 2
+NARROW_STEPS = 4
 PSUM_MAX_STEPS = 3
 EARLY_STEPS = 5
-BORROWED = {"x_woven0": 3}
-TAB_FIRST = 512
-SHARED = {"xg": "wb_woven1"}
+X_LEAD = 2
+Y_LAG = 2
+EARLY_BLOCKS, LATE_BLOCKS = (0, 1), (2, 3)
 
 
 def load_scale_rows(queue, plane, rows):
@@ -56,7 +57,7 @@ def tile_list_htabg_max_gateL_kernel(
         banks_taken = []
 
         def tile(name, shape, dtype, tag=None):
-            return keep.tile(shape, dtype, name=name, tag=tag or SHARED.get(name, name), align_bytes=256)
+            return keep.tile(shape, dtype, name=name, tag=tag or name, align_bytes=256)
 
         def next_bank():
             banks_taken.append(None)
@@ -84,6 +85,7 @@ def tile_list_htabg_max_gateL_kernel(
         tab_rows = tab_words[0].rearrange("p t i -> p (t i)").bitcast(I32)
         identity = tile("identity", [P, P], F32)
         make_identity(nc, identity[:])
+
         nc.sync.dma_start(
             out=wgt_rows[:],
             in_=wgt2.rearrange("(e s) j -> e s j", s=WGT_COPIES)[:, 0, :].rearrange("e (u c) -> e u c", c=P),
@@ -95,16 +97,14 @@ def tile_list_htabg_max_gateL_kernel(
         load_scale_rows(nc.sync, wa_s_raw, wa_scales)
         nc.sync.dma_start(idx2[:], offs2)
         nc.sync.dma_start(out=wb_raw[:], in_=wb.rearrange("(p i) r -> p i r", i=PACK))
-        nc.sync.dma_start(out=x_planes[0][:], in_=x_rows[:, 0, :])
-        nc.sync.dma_start(out=x_planes[1][:], in_=x_rows[:, 1, :])
+        for i in (0, 1):
+            nc.sync.dma_start(out=x_planes[i][:], in_=x_rows[:, i, :])
         load_scale_rows(nc.sync, wd_s, wd_scales)
-        nc.sync.dma_start(out=x_planes[2][:], in_=x_rows[:, 2, :])
-        nc.sync.dma_start(out=x_planes[3][:], in_=x_rows[:, 3, :])
+        for i in (2, 3):
+            nc.sync.dma_start(out=x_planes[i][:], in_=x_rows[:, i, :])
         nc.sync.dma_start(out=wd_w[:].bitcast(I32), in_=wd_words[0].bitcast(I32))
-        nc.sync.dma_start(out=gates[0][:], in_=gT[0 * P : 1 * P, :])
-        nc.sync.dma_start(out=gates[1][:], in_=gT[1 * P : 2 * P, :])
-        nc.sync.dma_start(out=gates[2][:], in_=gT[2 * P : 3 * P, :])
-        nc.sync.dma_start(out=gates[3][:], in_=gT[3 * P : 4 * P, :])
+        for b in range(OUT_BLOCKS):
+            nc.sync.dma_start(out=gates[b][:], in_=gT[b * P : (b + 1) * P, :])
 
         turned = next_bank()
         nc.tensor.transpose(turned[:, 0, :], wgt_rows[:], identity[:])
@@ -164,10 +164,11 @@ def tile_list_htabg_max_gateL_kernel(
         steps = [(sum(STEPS[:step]), width) for step, width in enumerate(STEPS)]
         y = [tile(f"y{half}", [P, OUT_BLOCKS, HALF], F32) for half in range(2)]
         yb = [tile(f"yb{step}", [P, width, PACK], BF16) for step, width in enumerate(STEPS)]
-        xg = tile("xg", [P, PACK * J], F32)[:].rearrange("p (i j) -> p i j", i=PACK)
+        xg = tile("xg", [P, PACK * J], F32, "wb_woven1")[:].rearrange("p (i j) -> p i j", i=PACK)
 
         wa_w = tile("wa_w", [P, R], I32)
         wa_s = tile("wa_s", [P, R], U8)
+
         def deal(copy, ordered, raw):
             copy(out=ordered.rearrange("p (t m) -> p t m", t=PACK), in_=raw.rearrange("p (m t) -> p t m", t=PACK))
 
@@ -175,7 +176,7 @@ def tile_list_htabg_max_gateL_kernel(
         deal(nc.vector.tensor_copy, wa_w[:].bitcast(U32), wa_w_raw[:].bitcast(U32))
 
         v_w = tile("v_w", [P, J], U32)
-        nc.vector.tensor_copy(v_w[:, 0:1024], tab_w[:].bitcast(U32).indirect(entries(idx, 0, 1024)))
+        nc.vector.tensor_copy(v_w[:, 0:J], tab_w[:].bitcast(U32).indirect(entries(idx, 0, J)))
         for step, (j0, width) in enumerate(steps):
             for u in range(0, width, BANK_J):
                 cols = slice(j0 + u, j0 + u + BANK_J)
@@ -186,13 +187,12 @@ def tile_list_htabg_max_gateL_kernel(
             cols = slice(j0, j0 + count)
             nc.vector.tensor_tensor(xg[:, i, cols], x_planes[i][:].indirect(entries(idx2, j0, count)), wgt[:, cols], MULT)
 
-        def bf16_tile(name, width):
-            if name in BORROWED:
-                plane, quarter = divmod(BORROWED[name], PACK)
-                return xg[:, PACK - 1 - plane, quarter * QUARTER : (quarter + 1) * QUARTER].bitcast(BF16)
+        def woven_tile(name, width):
             return tile(name, [P, width * PACK], BF16)[:]
 
-        x_woven = {step: bf16_tile(f"x_woven{step}", STEPS[step]) for step in range(EARLY_STEPS)}
+        x_woven = {0: xg[:, PACK - 1, 3 * QUARTER : 4 * QUARTER].bitcast(BF16)}
+        for step in range(1, EARLY_STEPS):
+            x_woven[step] = woven_tile(f"x_woven{step}", STEPS[step])
 
         def weave(step, first, count):
             j0, width = steps[step]
@@ -210,28 +210,30 @@ def tile_list_htabg_max_gateL_kernel(
 
         def make_xg(step):
             j0, width = steps[step]
+            if j0 % QUARTER == 0:
+                pick(PACK - 1, j0, QUARTER)
             if step < EARLY_STEPS:
                 weave(step, 2, 2)
             else:
-                x_woven[step] = bf16_tile(f"x_woven{step}", width)
+                x_woven[step] = woven_tile(f"x_woven{step}", width)
                 weave(step, 0, PACK)
             woven = x_woven[step].rearrange("p (j i) -> p j i", i=PACK)
             return quantise(f"xq{step}", woven)
 
         def make_h(step, x_w, x_s):
             width = STEPS[step]
-            banks = [slice(u, u + BANK_J) for u in range(0, width, BANK_J)]
-            h = bf16_tile(f"h{step}", width).rearrange("p (j t) -> p j t", t=PACK)
+            bank_columns = [slice(u, u + BANK_J) for u in range(0, width, BANK_J)]
+            h = woven_tile(f"h{step}", width).rearrange("p (j t) -> p j t", t=PACK)
             if step < PSUM_MAX_STEPS:
-                for cols in banks:
+                for cols in bank_columns:
                     ya_sums = first_layer(wa_w, wa_s, x_w[:, cols], x_s[:, cols])
                     nc.vector.tensor_tensor(h[:, cols, :], ya_sums, yb[step][:, cols, :], MAX)
             else:
                 ya = tile(f"ya{step}", [P, width, PACK], BF16)
-                for cols in banks:
+                for cols in bank_columns:
                     nc.scalar.copy(out=ya[:, cols, :], in_=first_layer(wa_w, wa_s, x_w[:, cols], x_s[:, cols]))
                 nc.vector.tensor_tensor(h, ya[:], yb[step][:], MAX)
-            return h
+            return quantise(f"hq{step}", h)
 
         def make_y(step, h_w, h_s):
             j0, width = steps[step]
@@ -257,49 +259,26 @@ def tile_list_htabg_max_gateL_kernel(
             if j0 + count == first + width:
                 nc.sync.dma_start(out=out[b * P : (b + 1) * P, first : first + width], in_=gated_tiles[b, first][:])
 
-        xq = {}
-        hv = {}
-        hq = {}
-        pick(3, 0, 256)
-        xq[0] = make_xg(0)
-        xq[1] = make_xg(1)
-        pick(3, 256, 256)
-        xq[2] = make_xg(2)
-        xq[3] = make_xg(3)
-        hv[0] = make_h(0, *xq[0])
-        hq[0] = quantise("hq0", hv[0])
-        hv[1] = make_h(1, *xq[1])
-        hq[1] = quantise("hq1", hv[1])
-        pick(3, 512, 256)
-        xq[4] = make_xg(4)
-        hv[2] = make_h(2, *xq[2])
-        hq[2] = quantise("hq2", hv[2])
-        make_y(0, *hq[0])
-        pick(3, 768, 256)
-        xq[5] = make_xg(5)
-        hv[3] = make_h(3, *xq[3])
-        hq[3] = quantise("hq3", hv[3])
-        make_y(1, *hq[1])
-        hv[4] = make_h(4, *xq[4])
-        hq[4] = quantise("hq4", hv[4])
-        make_y(2, *hq[2])
-        hv[5] = make_h(5, *xq[5])
-        hq[5] = quantise("hq5", hv[5])
-        make_y(3, *hq[3])
-        make_y(4, *hq[4])
-        make_y(5, *hq[5])
-        gate(0, 0, 128)
-        gate(0, 128, 128)
-        gate(1, 0, 256)
-        gate(0, 256, 128)
-        gate(1, 256, 128)
-        gate(0, 384, 128)
-        gate(1, 384, 128)
-        gate(2, 0, 512)
-        gate(0, 512, 256)
-        gate(1, 512, 384)
-        gate(3, 0, 512)
-        gate(2, 512, 512)
-        gate(3, 512, 512)
-        gate(0, 768, 256)
-        gate(1, 896, 128)
+        x_quantised = {step: make_xg(step) for step in range(NARROW_STEPS)}
+        h_quantised = {}
+        for step in range(len(STEPS)):
+            if NARROW_STEPS <= step + X_LEAD < len(STEPS):
+                x_quantised[step + X_LEAD] = make_xg(step + X_LEAD)
+            h_quantised[step] = make_h(step, *x_quantised[step])
+            if step >= Y_LAG:
+                make_y(step - Y_LAG, *h_quantised[step - Y_LAG])
+        for step in range(len(STEPS) - Y_LAG, len(STEPS)):
+            make_y(step, *h_quantised[step])
+
+        first_block, second_block = EARLY_BLOCKS
+        for j0, width in steps[:NARROW_STEPS]:
+            for b in EARLY_BLOCKS:
+                gate(b, j0, width)
+        gate(LATE_BLOCKS[0], 0, HALF)
+        gate(first_block, *steps[-2])
+        gate(second_block, HALF, HALF - BANK_J)
+        gate(LATE_BLOCKS[1], 0, HALF)
+        for b in LATE_BLOCKS:
+            gate(b, HALF, HALF)
+        gate(first_block, *steps[-1])
+        gate(second_block, J - BANK_J, BANK_J)

from contextlib import ExitStack

import concourse.mybir as mybir
from concourse.masks import make_identity

K, L, R, N, T, J = 512, 512, 512, 512, 2048, 1024
FLOPS = 2 * J * (K * R + L * R + R * N)

F32 = mybir.dt.float32
BF16 = mybir.dt.bfloat16
I32 = mybir.dt.int32
U32 = mybir.dt.uint32
U16 = mybir.dt.uint16
U8 = mybir.dt.uint8
FP8X4 = mybir.dt.float8_e4m3fn_x4
FP4X4 = mybir.dt.float4_e2m1fn_x4
MULT = mybir.AluOpType.mult
MAX = mybir.AluOpType.max

P = 128
PACK = 4
GROUP = 16
QUADRANTS = 4
BANKS = 8
BANK_J = 128
OUT_BLOCKS = N // P
WGT_BLOCKS = J // P
WGT_COPIES = 8
HALF, QUARTER = J // 2, J // 4

STEPS = (BANK_J,) * 4 + (QUARTER,) * 2
NARROW_STEPS = 4
PSUM_MAX_STEPS = 3
EARLY_STEPS = 5
X_LEAD = 2
Y_LAG = 2
EARLY_BLOCKS, LATE_BLOCKS = (0, 1), (2, 3)


def load_scale_rows(queue, plane, rows):
    for q in range(QUADRANTS):
        queue.dma_start(out=plane[32 * q : 32 * q + 4, :].bitcast(I32), in_=rows[0, 4 * q : 4 * q + 4, :].bitcast(I32))


def entries(offsets, j0, count):
    return offsets[:, j0 // GROUP : (j0 + count) // GROUP]


def tile_list_htabg_max_gateL_kernel(
    tc, tab_words, tab_scales, xT, wgt2, wa_words, wa_scales, wb, wd_words, wd_scales, gT, offs, offs2, out
):
    nc = tc.nc
    with ExitStack() as ctx:
        lists = ctx.enter_context(tc.tile_pool(name="lists", bufs=1))
        keep = ctx.enter_context(tc.tile_pool(name="keep", bufs=1))
        psum = ctx.enter_context(tc.psum_pool(name="psum", bufs=1))
        banks_taken = []

        def tile(name, shape, dtype, tag=None):
            return keep.tile(shape, dtype, name=name, tag=tag or name, align_bytes=256)

        def next_bank():
            banks_taken.append(None)
            return psum.tile([P, PACK, BANK_J], F32, name=f"bank{len(banks_taken) % BANKS}")

        idx = lists.tile([P, J // GROUP], U16, name="idx")
        idx2 = lists.tile([P, J // GROUP], U16, name="idx2")

        tab_s = tile("tab_s", [P, T], U8)
        wa_s_raw = tile("wa_s_raw", [P, R], U8)
        wd_s = tile("wd_s", [P, N], U8)
        for plane in (tab_s, wa_s_raw, wd_s):
            nc.vector.memset(plane[:].bitcast(I32), 0)

        wa_w_raw = tile("wa_w_raw", [P, R], I32)
        wb_raw = tile("wb_raw", [P, PACK, R], F32)
        tab_w = tile("tab_w", [P, T], I32)
        wgt = tile("wgt", [P, J], F32)
        wgt_rows = tile("wgt_rows", [P, P], F32)
        wd_w = tile("wd_w", [P, 2 * N], U8)
        x_rows = xT.rearrange("(p i) t -> p i t", i=PACK)
        x_planes = [tile(f"x{i}", [P, T], F32) for i in range(PACK)]
        gates = [tile(f"g{b}", [P, T], F32) for b in range(OUT_BLOCKS)]

        tab_rows = tab_words[0].rearrange("p t i -> p (t i)").bitcast(I32)
        identity = tile("identity", [P, P], F32)
        make_identity(nc, identity[:])

        nc.sync.dma_start(
            out=wgt_rows[:],
            in_=wgt2.rearrange("(e s) j -> e s j", s=WGT_COPIES)[:, 0, :].rearrange("e (u c) -> e u c", c=P),
        )
        nc.sync.dma_start(out=wa_w_raw[:], in_=wa_words[0].rearrange("p r i -> p (r i)").bitcast(I32))
        nc.sync.dma_start(idx[:], offs)
        load_scale_rows(nc.sync, tab_s, tab_scales)
        nc.sync.dma_start(out=tab_w[:], in_=tab_rows)
        load_scale_rows(nc.sync, wa_s_raw, wa_scales)
        nc.sync.dma_start(idx2[:], offs2)
        nc.sync.dma_start(out=wb_raw[:], in_=wb.rearrange("(p i) r -> p i r", i=PACK))
        for i in (0, 1):
            nc.sync.dma_start(out=x_planes[i][:], in_=x_rows[:, i, :])
        load_scale_rows(nc.sync, wd_s, wd_scales)
        for i in (2, 3):
            nc.sync.dma_start(out=x_planes[i][:], in_=x_rows[:, i, :])
        nc.sync.dma_start(out=wd_w[:].bitcast(I32), in_=wd_words[0].bitcast(I32))
        for b in range(OUT_BLOCKS):
            nc.sync.dma_start(out=gates[b][:], in_=gT[b * P : (b + 1) * P, :])

        turned = next_bank()
        nc.tensor.transpose(turned[:, 0, :], wgt_rows[:], identity[:])
        spread = tile("spread", [P, WGT_BLOCKS, P // WGT_COPIES, WGT_COPIES], F32)
        nc.scalar.copy(
            out=spread[:],
            in_=turned[:, 0, :]
            .rearrange("c (row u) -> c u row", u=WGT_BLOCKS)
            .unsqueeze(3)
            .to_broadcast([P, WGT_BLOCKS, P // WGT_COPIES, WGT_COPIES]),
        )
        for u0 in range(0, WGT_BLOCKS, PACK):
            back = next_bank()
            for u in range(PACK):
                nc.tensor.transpose(back[:, u, :], spread[:, u0 + u, :, :].rearrange("c row a -> c (row a)"), identity[:])
            nc.scalar.copy(out=wgt[:, u0 * P : (u0 + PACK) * P], in_=back[:].rearrange("p u c -> p (u c)"))

        v_s = tile("v_s", [P, J], U8)
        nc.vector.tensor_copy(v_s[:], tab_s[:].indirect(idx[:]))

        wb_w = tile("wb_w", [P, R], U32)
        wb_s = tile("wb_s", [P, R], U8)
        for half, (copy, tag) in enumerate(((nc.scalar.copy, "spread"), (nc.vector.tensor_copy, None))):
            wb_woven = tile(f"wb_woven{half}", [P, R // 2 * PACK], BF16, tag)
            copy(
                out=wb_woven[:].rearrange("p (t m i) -> p m i t", t=2, i=PACK),
                in_=wb_raw[:].rearrange("p i (m t) -> p m i t", t=PACK)[:, :, :, 2 * half : 2 * half + 2],
            )
            dealt = slice(half * R // 2, (half + 1) * R // 2)
            nc.vector.quantize_mx(out=wb_w[:, dealt].bitcast(FP8X4), scales=wb_s[:, dealt], in_=wb_woven[:])

        def product(stationary, stationary_scales, words, scales):
            bank = next_bank()
            for u in range(PACK):
                nc.tensor.matmul_mx(
                    out=bank[:, u, :],
                    lhsT=stationary(u),
                    lhsT_scale=stationary_scales[:, u * P : (u + 1) * P],
                    rhs=words.bitcast(FP8X4),
                    rhs_scale=scales,
                    start=True,
                    stop=True,
                )
            return bank

        def first_layer(w_words, w_scales, words, scales):
            bank = product(lambda t: w_words[:, t * P : (t + 1) * P].bitcast(FP8X4), w_scales, words, scales)
            return bank[:].rearrange("p t j -> p j t")

        def quantise(name, woven):
            width = woven.shape[1]
            words = tile(name + "_w", [P, width], U32)
            scales = tile(name + "_s", [P, width], U8)
            nc.vector.quantize_mx(out=words[:].bitcast(FP8X4), scales=scales[:], in_=woven.rearrange("p j t -> p (j t)"))
            return words, scales

        steps = [(sum(STEPS[:step]), width) for step, width in enumerate(STEPS)]
        y = [tile(f"y{half}", [P, OUT_BLOCKS, HALF], F32) for half in range(2)]
        yb = [tile(f"yb{step}", [P, width, PACK], BF16) for step, width in enumerate(STEPS)]
        xg = tile("xg", [P, PACK * J], F32, "wb_woven1")[:].rearrange("p (i j) -> p i j", i=PACK)

        wa_w = tile("wa_w", [P, R], I32)
        wa_s = tile("wa_s", [P, R], U8)

        def deal(copy, ordered, raw):
            copy(out=ordered.rearrange("p (t m) -> p t m", t=PACK), in_=raw.rearrange("p (m t) -> p t m", t=PACK))

        deal(nc.gpsimd.tensor_copy, wa_s[:], wa_s_raw[:])
        deal(nc.vector.tensor_copy, wa_w[:].bitcast(U32), wa_w_raw[:].bitcast(U32))

        v_w = tile("v_w", [P, J], U32)
        nc.vector.tensor_copy(v_w[:, 0:J], tab_w[:].bitcast(U32).indirect(entries(idx, 0, J)))
        for step, (j0, width) in enumerate(steps):
            for u in range(0, width, BANK_J):
                cols = slice(j0 + u, j0 + u + BANK_J)
                sums = first_layer(wb_w, wb_s, v_w[:, cols], v_s[:, cols])
                nc.scalar.copy(out=yb[step][:, u : u + BANK_J, :], in_=sums)

        def pick(i, j0, count):
            cols = slice(j0, j0 + count)
            nc.vector.tensor_tensor(xg[:, i, cols], x_planes[i][:].indirect(entries(idx2, j0, count)), wgt[:, cols], MULT)

        def woven_tile(name, width):
            return tile(name, [P, width * PACK], BF16)[:]

        x_woven = {0: xg[:, PACK - 1, 3 * QUARTER : 4 * QUARTER].bitcast(BF16)}
        for step in range(1, EARLY_STEPS):
            x_woven[step] = woven_tile(f"x_woven{step}", STEPS[step])

        def weave(step, first, count):
            j0, width = steps[step]
            planes = slice(first, first + count)
            nc.scalar.copy(
                out=x_woven[step].rearrange("p (u v i) -> p u i v", v=4, i=PACK)[:, :, planes, :],
                in_=xg[:, planes, j0 : j0 + width].rearrange("p i (u v) -> p u i v", v=4),
            )

        for i in range(PACK - 1):
            pick(i, 0, J)
            if i == 1:
                for step in range(EARLY_STEPS):
                    weave(step, 0, 2)

        def make_xg(step):
            j0, width = steps[step]
            if j0 % QUARTER == 0:
                pick(PACK - 1, j0, QUARTER)
            if step < EARLY_STEPS:
                weave(step, 2, 2)
            else:
                x_woven[step] = woven_tile(f"x_woven{step}", width)
                weave(step, 0, PACK)
            woven = x_woven[step].rearrange("p (j i) -> p j i", i=PACK)
            return quantise(f"xq{step}", woven)

        def make_h(step, x_w, x_s):
            width = STEPS[step]
            bank_columns = [slice(u, u + BANK_J) for u in range(0, width, BANK_J)]
            h = woven_tile(f"h{step}", width).rearrange("p (j t) -> p j t", t=PACK)
            if step < PSUM_MAX_STEPS:
                for cols in bank_columns:
                    ya_sums = first_layer(wa_w, wa_s, x_w[:, cols], x_s[:, cols])
                    nc.vector.tensor_tensor(h[:, cols, :], ya_sums, yb[step][:, cols, :], MAX)
            else:
                ya = tile(f"ya{step}", [P, width, PACK], BF16)
                for cols in bank_columns:
                    nc.scalar.copy(out=ya[:, cols, :], in_=first_layer(wa_w, wa_s, x_w[:, cols], x_s[:, cols]))
                nc.vector.tensor_tensor(h, ya[:], yb[step][:], MAX)
            return quantise(f"hq{step}", h)

        def make_y(step, h_w, h_s):
            j0, width = steps[step]
            for u in range(0, width, BANK_J):
                cols = slice(u, u + BANK_J)
                bank = product(
                    lambda b: wd_w[:, 2 * b * P : 2 * (b + 1) * P].bitcast(FP4X4), wd_s, h_w[:, cols], h_s[:, cols]
                )
                at = (j0 + u) % HALF
                nc.scalar.copy(out=y[j0 // HALF][:, :, at : at + BANK_J], in_=bank[:])

        gated_tiles = {}

        def gate(b, j0, count):
            width = max(count, QUARTER) if j0 < HALF else count
            first = j0 - j0 % QUARTER if j0 < HALF else j0
            if j0 == first:
                gated_tiles[b, first] = tile(f"gated{b}_{j0}", [P, width], F32)
            gated = gated_tiles[b, first][:, j0 - first : j0 - first + count]
            at = j0 % HALF
            sums = y[j0 // HALF][:, b, at : at + count]
            nc.vector.tensor_tensor(gated, gates[b][:].indirect(entries(idx, j0, count)), sums, MULT)
            if j0 + count == first + width:
                nc.sync.dma_start(out=out[b * P : (b + 1) * P, first : first + width], in_=gated_tiles[b, first][:])

        x_quantised = {step: make_xg(step) for step in range(NARROW_STEPS)}
        h_quantised = {}
        for step in range(len(STEPS)):
            if NARROW_STEPS <= step + X_LEAD < len(STEPS):
                x_quantised[step + X_LEAD] = make_xg(step + X_LEAD)
            h_quantised[step] = make_h(step, *x_quantised[step])
            if step >= Y_LAG:
                make_y(step - Y_LAG, *h_quantised[step - Y_LAG])
        for step in range(len(STEPS) - Y_LAG, len(STEPS)):
            make_y(step, *h_quantised[step])

        first_block, second_block = EARLY_BLOCKS
        for j0, width in steps[:NARROW_STEPS]:
            for b in EARLY_BLOCKS:
                gate(b, j0, width)
        gate(LATE_BLOCKS[0], 0, HALF)
        gate(first_block, *steps[-2])
        gate(second_block, HALF, HALF - BANK_J)
        gate(LATE_BLOCKS[1], 0, HALF)
        for b in LATE_BLOCKS:
            gate(b, HALF, HALF)
        gate(first_block, *steps[-1])
        gate(second_block, J - BANK_J, BANK_J)
